import numpy as np
import ml_dtypes


def mxq(x, axis, fmt="e4m3"):
    dtype, down = {"e4m3": (ml_dtypes.float8_e4m3fn, 7), "e5m2": (ml_dtypes.float8_e5m2, 14)}[fmt]
    v = np.moveaxis(np.asarray(x, np.float32).astype(ml_dtypes.bfloat16).astype(np.float64), axis, -1)
    blocks = v.reshape(v.shape[:-1] + (-1, 32))
    amax = np.abs(blocks).max(-1, keepdims=True)
    byte = np.maximum(np.where(amax > 0, np.frexp(amax)[1] - 1 + 127, 0) - down, 1)
    scale = np.exp2(byte - 127.0)
    codes = (blocks / scale).astype(np.float32).astype(dtype).astype(np.float64)
    return np.moveaxis((codes * scale).reshape(v.shape), -1, axis)


WIDE = False


def mx_kscale(k, group=512):
    if not WIDE:
        return np.ones(k)
    levels = np.array([10, -10, 5, -5, 0])
    if group != 512:
        return np.exp2(np.random.permutation(np.resize(levels, k // group))).repeat(group)
    if k % 512:
        return np.exp2(np.random.permutation(np.resize(levels, k // 32))).repeat(32)
    a = np.empty((k // 512, 16))
    for p in range(k // 512):
        a[p, :8] = np.random.permutation(np.resize(levels, 8))
        for g in range(8):
            far = levels[np.abs(levels - a[p, g]) >= 10]
            a[p, g + 8] = far[np.random.randint(len(far))]
    return np.exp2(a.ravel()).repeat(32)


def f64(x):
    return np.asarray(x).astype(np.float64)


def striped(idx):
    return np.tile(np.asarray(idx).reshape(-1, 16).T, (8, 1)).astype(np.uint16)


def unstriped(offs):
    return offs[:16].T.reshape(-1).astype(np.int64)


H, KV, D, NQ, N = 4, 2, 256, 512, 512


def setup_inputs():
    n = np.random.standard_normal
    s = mx_kscale(D, 0)[:, None]
    u = mx_kscale(N)
    t = np.random.uniform(0.5, 2.0, N) * u
    v = n((KV, N, 128))
    v[:, :, 127] = 1.0
    return {
        "qT": (n((H, D, NQ)) * s * (0.70 / np.sqrt(D))).astype(np.float32),
        "kT": (n((KV, D, N)) / s).astype(np.float32),
        "t": t.reshape(N, 1).astype(np.float32),
        "v": (v / t[:, None]).astype(np.float32),
        "kb": (0.5 * n((N, 1))).astype(np.float32),
        "sink": (N * np.random.uniform(0.1, 1.0, (H, NQ, 1))).astype(np.float32),
        "og": n((H, NQ, 128)).astype(np.float32),
    }


def reference(qT, kT, t, v, kb, sink, og):
    a = np.repeat(mxq(f64(kT), 1, "e4m3"), H // KV, 0).transpose(0, 2, 1) @ mxq(f64(qT), 1, "e4m3")
    a = a + f64(kb)
    p = np.exp(a)
    w = p * f64(t)
    y = mxq(w, 1, "e4m3").transpose(0, 2, 1) @ np.repeat(mxq(f64(v), 1, "e4m3"), H // KV, 0)
    y = y / (y[:, :, 127:128] + f64(sink))
    y = y / (1.0 + np.exp(-f64(og)))
    return y

@@ -1,0 +1,303 @@
+import math
+from contextlib import ExitStack
+
+import concourse.mybir as mybir
+
+H, KV, D, NQ, N, E = 4, 2, 256, 512, 512, 128
+FLOPS = 2 * H * N * NQ * (D + E)
+
+F32 = mybir.dt.float32
+BF16 = mybir.dt.bfloat16
+I32 = mybir.dt.int32
+U32 = mybir.dt.uint32
+U8 = mybir.dt.uint8
+FP8X4 = mybir.dt.float8_e4m3fn_x4
+ALU = mybir.AluOpType
+ACT = mybir.ActivationFunctionType
+
+P = 128
+ROWS = 64
+PACK = 4
+HALF = 256
+ONE_BITS = 0x3F800000
+MANTISSA = 0x007FFFFF
+SIGN_BIT = -0x80000000
+
+PAIRS = ((1, 2), (0, 3))
+UNITS = [(pair, half, g) for pair in range(2) for half in range(2) for g in range(2)]
+V_SHARE = 44
+
+
+def tile_rows_a_exp_kb_sink_gate_kernel(tc, qT, kT, t, v, kb, sink, og, out):
+    nc = tc.nc
+    with ExitStack() as ctx:
+        sb = ctx.enter_context(tc.tile_pool(name="sb", bufs=1))
+        ps = ctx.enter_context(tc.psum_pool(name="ps", bufs=1))
+        ctx.enter_context(tc.manual_schedule())
+
+        def tile(name, shape, dtype):
+            return sb.tile(shape, dtype, name=name, align_bytes=64)
+
+        def tiles(name, count, shape, dtype):
+            return [tile("%s%d" % (name, i), shape, dtype) for i in range(count)]
+
+        t_raw = tile("t_raw", [P, PACK], F32)
+        kb_raw = tile("kb_raw", [P, PACK], F32)
+        sink_raw = tile("sink_raw", [P, H, 2, 2], F32)
+        mant = tile("mant", [P, PACK], I32)
+        expo = tile("expo", [P, PACK], I32)
+        sign = tile("sign", [P, 1, PACK, 1], I32)
+        expo_ln = tile("expo_ln", [P, PACK], F32)
+        bias_part = tile("bias_part", [P, PACK], F32)
+        mant_ln = tile("mant_ln", [P, PACK], F32)
+        bias = tile("bias", [P, PACK], F32)
+        warm_in = tile("warm_in", [P, 1], F32)
+        warm_out = tiles("warm_out", 2, [P, 1], F32)
+
+        k_raw = tiles("k_raw", 2, [P, PACK, HALF], F32)
+        k_bf = tile("k_bf", [P, PACK, P, PACK], BF16)
+        k_codes = tile("k_codes", [P, N], U32)
+        k_scales = tile("k_scales", [P, N], U8)
+        qa_raw = tiles("qa_raw", 2, [P, PACK, HALF], F32)
+        qb_raw = tile("qb_raw", [P, PACK, NQ], F32)
+        q_bf = tiles("q_bf", 4, [P, 2, P, PACK], BF16)
+        q_codes = tiles("q_codes", 4, [P, HALF], U32)
+        q_scales = tiles("q_scales", 4, [P, HALF], U8)
+        v_raw = tile("v_raw", [P, KV, PACK, E], F32)
+        v_bf = tile("v_bf", [P, KV, E, PACK], BF16)
+        v_codes = tile("v_codes", [P, KV * E], U32)
+        v_scales = tile("v_scales", [P, KV * E], U8)
+        og_raw = tiles("og_raw", H, [P, 2, 2 * E], F32)
+        w_rows = tiles("w_rows", 8, [P, PACK, HALF], BF16)
+        w_bf = tiles("w_bf", 8, [P, HALF, PACK], BF16)
+        w_codes = tiles("w_codes", 8, [P, HALF], U32)
+        w_scales = tiles("w_scales", 8, [P, HALF], U8)
+        tanh = tiles("tanh", 8, [P, 2 * E], F32)
+        gate = tiles("gate", 8, [P, 2 * E], F32)
+        den = tiles("den", 8, [P, 2], F32)
+        rden = tiles("rden", 8, [P, 2], F32)
+        res = tiles("res", 8, [P, 2, E], F32)
+
+        score = [[ps.tile([P, 2, HALF], F32, name="score%d%d" % (g, b)) for b in range(2)] for g in range(2)]
+        y = [ps.tile([P, 4, E], F32, name="y%d" % b) for b in range(4)]
+
+        def head_of(i):
+            pair, half, g = UNITS[i]
+            return PAIRS[pair][g]
+
+        nc.scalar.dma_start(out=t_raw[:], in_=t.rearrange("(p j) o -> p (j o)", j=PACK))
+        nc.scalar.dma_start(out=kb_raw[:], in_=kb.rearrange("(p j) o -> p (j o)", j=PACK))
+        k_view = kT.rearrange("g (p j) n -> (g p) j n", j=PACK)
+        qa_view = qT[1:3].rearrange("g (p j) n -> (g p) j n", j=PACK)
+        for a in range(2):
+            nc.sync.dma_start(out=k_raw[a][:], in_=k_view[:, :, a * HALF : (a + 1) * HALF])
+        for a in range(2):
+            nc.sync.dma_start(out=qa_raw[a][:], in_=qa_view[:, :, a * HALF : (a + 1) * HALF])
+        nc.sync.dma_start(
+            out=v_raw[:].rearrange("p g j e -> p g (j e)"),
+            in_=v.rearrange("g (p j) e -> p g (j e)", j=PACK),
+        )
+        nc.sync.dma_start(out=qb_raw[0:ROWS], in_=qT[0].rearrange("(p j) n -> p j n", j=PACK))
+        nc.sync.dma_start(
+            out=sink_raw[:].rearrange("p h u c -> p (h u) c"),
+            in_=sink.rearrange("h (u m c) o -> m (h u) (c o)", u=2, c=2),
+        )
+        for h in (1, 2, 0, 3):
+            nc.sync.dma_start(out=og_raw[h][:], in_=og[h].rearrange("(u m c) e -> m u (c e)", u=2, c=2))
+
+        def cast_k(a):
+            nc.vector.tensor_copy(
+                out=k_bf[:, :, a * ROWS : (a + 1) * ROWS, :].rearrange("p r s j -> p s j r"),
+                in_=k_raw[a][:].rearrange("p j (s r) -> p s j r", r=PACK),
+            )
+
+        def cast_q(n, copy, lo, hi):
+            raw = qa_raw[n][:] if n < 2 else qb_raw[:, :, (n - 2) * HALF : (n - 1) * HALF]
+            copy(
+                out=q_bf[n][:].rearrange("p c (a b) j -> p a j b c", b=2)[:, lo:hi],
+                in_=raw.rearrange("p j (a b c) -> p a j b c", b=2, c=2)[:, lo:hi],
+            )
+
+        def quantize(codes, scales, grouped):
+            nc.vector.quantize_mx(out=codes[:].bitcast(FP8X4), scales=scales[:], in_=grouped)
+
+        def quant_q(n):
+            quantize(q_codes[n], q_scales[n], q_bf[n][:].rearrange("p c m j -> p (c m j)"))
+
+        def cast_v(g):
+            nc.vector.tensor_tensor(
+                out=v_bf[:, g].rearrange("p (a b) j -> p a j b", b=PACK),
+                in0=v_raw[:, g].rearrange("p j (a b) -> p a j b", b=PACK),
+                in1=sign[:].bitcast(F32).to_broadcast([P, E // PACK, PACK, PACK]),
+                op=ALU.mult,
+            )
+
+        def scores(i):
+            pair, half, g = UNITS[i]
+            n = 2 * pair + half
+            rows = slice(g * ROWS, (g + 1) * ROWS)
+            for r in range(PACK):
+                for c in range(2):
+                    tok = slice(r * P, (r + 1) * P)
+                    qs = slice(c * P, (c + 1) * P)
+                    nc.tensor.matmul_mx(
+                        out=score[g][r // 2][:, r % 2, qs],
+                        lhsT=k_codes[rows, tok].bitcast(FP8X4),
+                        lhsT_scale=k_scales[rows, tok],
+                        rhs=q_codes[n][rows, qs].bitcast(FP8X4),
+                        rhs_scale=q_scales[n][rows, qs],
+                        start=True,
+                        stop=True,
+                    )
+
+        def weights(i):
+            g = UNITS[i][2]
+            for r in range(PACK):
+                nc.scalar.activation(
+                    out=w_rows[i][:, r, :], in_=score[g][r // 2][:, r % 2, :], func=ACT.Exp, bias=bias[:, r : r + 1]
+                )
+
+        def group_w(i):
+            nc.vector.tensor_copy(
+                out=w_bf[i][:].rearrange("p (a b) r -> p a r b", b=PACK),
+                in_=w_rows[i][:].rearrange("p r (a b) -> p a r b", b=PACK),
+            )
+
+        def quant_w(i):
+            quantize(w_codes[i], w_scales[i], w_bf[i][:].rearrange("p q r -> p (q r)"))
+
+        def values(i):
+            g = UNITS[i][2]
+            feats = slice(g * E, (g + 1) * E)
+            for c in range(2):
+                qs = slice(c * P, (c + 1) * P)
+                nc.tensor.matmul_mx(
+                    out=y[i % 4][:, c, :],
+                    lhsT=w_codes[i][:, qs].bitcast(FP8X4),
+                    lhsT_scale=w_scales[i][:, qs],
+                    rhs=v_codes[:, feats].bitcast(FP8X4),
+                    rhs_scale=v_scales[:, feats],
+                    start=True,
+                    stop=True,
+                )
+
+        def gate_tanh(i):
+            nc.scalar.activation(out=tanh[i][:], in_=og_raw[head_of(i)][:, UNITS[i][1], :], func=ACT.Tanh, scale=0.5)
+
+        def gate_vector(i):
+            nc.vector.tensor_scalar(
+                out=gate[i][:], in0=tanh[i][:], scalar1=0.5, scalar2=0.5, op0=ALU.mult, op1=ALU.add
+            )
+
+        def gate_scalar(i):
+            nc.scalar.activation(out=gate[i][:], in_=tanh[i][:], func=ACT.Copy, scale=0.5, bias=0.5)
+
+        def denominator(i):
+            nc.vector.tensor_tensor(
+                out=den[i][:], in0=y[i % 4][:, 0:2, E - 1], in1=sink_raw[:, head_of(i), UNITS[i][1], :], op=ALU.add
+            )
+
+        def invert(i):
+            nc.vector.reciprocal(out=rden[i][:], in_=den[i][:])
+
+        def finish(i):
+            for c in range(2):
+                nc.vector.scalar_tensor_tensor(
+                    out=res[i][:, c, :],
+                    in0=y[i % 4][:, c, :],
+                    scalar=rden[i][:, c : c + 1],
+                    in1=gate[i][:, c * E : (c + 1) * E],
+                    op0=ALU.mult,
+                    op1=ALU.mult,
+                )
+            half = UNITS[i][1]
+            nc.sync.dma_start(
+                out=out[head_of(i), half * HALF : (half + 1) * HALF, :].rearrange("(m c) e -> m c e", c=2),
+                in_=res[i][:],
+            )
+
+        nc.gpsimd.memset(warm_in[:], 1.0)
+        nc.scalar.activation(out=warm_out[0][:], in_=warm_in[:], func=ACT.Ln)
+        t_bits = t_raw[:].bitcast(I32)
+        nc.vector.tensor_scalar(
+            out=mant[:], in0=t_bits, scalar1=MANTISSA, scalar2=ONE_BITS, op0=ALU.bitwise_and, op1=ALU.bitwise_or
+        )
+        nc.vector.tensor_scalar(
+            out=expo[:], in0=t_bits, scalar1=23, scalar2=0xFF, op0=ALU.logical_shift_right, op1=ALU.bitwise_and
+        )
+        nc.vector.tensor_scalar(
+            out=sign[:, 0, :, 0], in0=t_bits, scalar1=SIGN_BIT, scalar2=ONE_BITS, op0=ALU.bitwise_and, op1=ALU.bitwise_or
+        )
+        nc.scalar.activation(out=mant_ln[:], in_=mant[:].bitcast(F32), func=ACT.Ln)
+        nc.scalar.activation(out=warm_out[1][:], in_=warm_in[:], func=ACT.Exp)
+        nc.vector.tensor_scalar(
+            out=expo_ln[:], in0=expo[:], scalar1=-127.0, scalar2=math.log(2.0), op0=ALU.add, op1=ALU.mult
+        )
+        cast_k(0)
+        nc.vector.tensor_tensor(out=bias_part[:], in0=expo_ln[:], in1=kb_raw[:], op=ALU.add)
+        cast_k(1)
+        nc.vector.tensor_tensor(out=bias[:], in0=bias_part[:], in1=mant_ln[:], op=ALU.add)
+        quantize(k_codes, k_scales, k_bf[:].rearrange("p r s j -> p (r s j)"))
+        cast_q(0, nc.vector.tensor_copy, 0, V_SHARE)
+        cast_q(0, nc.scalar.copy, V_SHARE, 64)
+        quant_q(0)
+        scores(0)
+        scores(1)
+        cast_q(1, nc.scalar.copy, V_SHARE, 64)
+        cast_q(1, nc.vector.tensor_copy, 0, V_SHARE)
+        weights(0)
+        nc.scalar.dma_start(out=qb_raw[ROWS:P], in_=qT[3].rearrange("(p j) n -> p j n", j=PACK))
+        cast_v(0)
+        quant_q(1)
+        scores(2)
+        cast_v(1)
+        weights(1)
+        scores(3)
+        group_w(0)
+        quantize(v_codes, v_scales, v_bf[:].rearrange("p g e j -> p (g e j)"))
+        quant_w(0)
+        values(0)
+        cast_q(2, nc.vector.tensor_copy, 0, 64)
+        group_w(1)
+        quant_q(2)
+        weights(2)
+        scores(4)
+        quant_w(1)
+        values(1)
+        weights(3)
+        scores(5)
+        group_w(2)
+        cast_q(3, nc.vector.tensor_copy, 0, 64)
+        quant_w(2)
+        values(2)
+        quant_q(3)
+        gate_tanh(0)
+        gate_tanh(1)
+        for i in range(3, 8):
+            if i + 1 < 8:
+                weights(i + 1)
+                if i + 3 < 8:
+                    scores(i + 3)
+                gate_tanh(i - 1)
+            if i == 7:
+                gate_tanh(6)
+                gate_tanh(7)
+                gate_scalar(6)
+                gate_scalar(7)
+            denominator(i - 3)
+            group_w(i)
+            invert(i - 3)
+            gate_vector(i - 3)
+            quant_w(i)
+            finish(i - 3)
+            values(i)
+        denominator(5)
+        denominator(6)
+        gate_vector(5)
+        invert(5)
+        invert(6)
+        denominator(7)
+        finish(5)
+        invert(7)
+        finish(6)
+        finish(7)

@@ -25,7 +25,6 @@ SIGN_BIT = -0x80000000
 
 PAIRS = ((1, 2), (0, 3))
 UNITS = [(pair, half, g) for pair in range(2) for half in range(2) for g in range(2)]
-V_SHARE = 44
 
 
 def tile_rows_a_exp_kb_sink_gate_kernel(tc, qT, kT, t, v, kb, sink, og, out):
@@ -46,7 +45,7 @@ def tile_rows_a_exp_kb_sink_gate_kernel(tc, qT, kT, t, v, kb, sink, og, out):
         sink_raw = tile("sink_raw", [P, H, 2, 2], F32)
         mant = tile("mant", [P, PACK], I32)
         expo = tile("expo", [P, PACK], I32)
-        sign = tile("sign", [P, 1, PACK, 1], I32)
+        sign = tile("sign", [P, 1, 1, PACK], I32)
         expo_ln = tile("expo_ln", [P, PACK], F32)
         bias_part = tile("bias_part", [P, PACK], F32)
         mant_ln = tile("mant_ln", [P, PACK], F32)
@@ -60,7 +59,7 @@ def tile_rows_a_exp_kb_sink_gate_kernel(tc, qT, kT, t, v, kb, sink, og, out):
         k_scales = tile("k_scales", [P, N], U8)
         qa_raw = tiles("qa_raw", 2, [P, PACK, HALF], F32)
         qb_raw = tile("qb_raw", [P, PACK, NQ], F32)
-        q_bf = tiles("q_bf", 4, [P, 2, P, PACK], BF16)
+        q_bf = tiles("q_bf", 4, [P, HALF, PACK], BF16)
         q_codes = tiles("q_codes", 4, [P, HALF], U32)
         q_scales = tiles("q_scales", 4, [P, HALF], U8)
         v_raw = tile("v_raw", [P, KV, PACK, E], F32)
@@ -72,14 +71,14 @@ def tile_rows_a_exp_kb_sink_gate_kernel(tc, qT, kT, t, v, kb, sink, og, out):
         w_bf = tiles("w_bf", 8, [P, HALF, PACK], BF16)
         w_codes = tiles("w_codes", 8, [P, HALF], U32)
         w_scales = tiles("w_scales", 8, [P, HALF], U8)
-        tanh = tiles("tanh", 8, [P, 2 * E], F32)
-        gate = tiles("gate", 8, [P, 2 * E], F32)
-        den = tiles("den", 8, [P, 2], F32)
-        rden = tiles("rden", 8, [P, 2], F32)
+        tanh = tiles("tanh", H, [P, 2, 2 * E], F32)
+        gate = tiles("gate", H, [P, 2, 2 * E], F32)
+        den = tiles("den", 5, [P, 2, 2], F32)
+        rden = tiles("rden", 5, [P, 2, 2], F32)
         res = tiles("res", 8, [P, 2, E], F32)
 
         score = [[ps.tile([P, 2, HALF], F32, name="score%d%d" % (g, b)) for b in range(2)] for g in range(2)]
-        y = [ps.tile([P, 4, E], F32, name="y%d" % b) for b in range(4)]
+        y = [ps.tile([P, 2, 2, E], F32, name="y%d" % b) for b in range(4)]
 
         def head_of(i):
             pair, half, g = UNITS[i]
@@ -89,82 +88,103 @@ def tile_rows_a_exp_kb_sink_gate_kernel(tc, qT, kT, t, v, kb, sink, og, out):
         nc.scalar.dma_start(out=kb_raw[:], in_=kb.rearrange("(p j) o -> p (j o)", j=PACK))
         k_view = kT.rearrange("g (p j) n -> (g p) j n", j=PACK)
         qa_view = qT[1:3].rearrange("g (p j) n -> (g p) j n", j=PACK)
+        nc.sync.dma_start(out=qa_raw[0][:], in_=qa_view[:, :, 0:HALF])
         for a in range(2):
             nc.sync.dma_start(out=k_raw[a][:], in_=k_view[:, :, a * HALF : (a + 1) * HALF])
-        for a in range(2):
-            nc.sync.dma_start(out=qa_raw[a][:], in_=qa_view[:, :, a * HALF : (a + 1) * HALF])
+        nc.sync.dma_start(out=qa_raw[1][:], in_=qa_view[:, :, HALF:NQ])
         nc.sync.dma_start(
             out=v_raw[:].rearrange("p g j e -> p g (j e)"),
             in_=v.rearrange("g (p j) e -> p g (j e)", j=PACK),
         )
         nc.sync.dma_start(out=qb_raw[0:ROWS], in_=qT[0].rearrange("(p j) n -> p j n", j=PACK))
+
+        def load_og(h):
+            nc.sync.dma_start(out=og_raw[h][:], in_=og[h].rearrange("(u m c) e -> m u (c e)", u=2, c=2))
+
+        load_og(1)
+        load_og(2)
         nc.sync.dma_start(
             out=sink_raw[:].rearrange("p h u c -> p (h u) c"),
             in_=sink.rearrange("h (u m c) o -> m (h u) (c o)", u=2, c=2),
         )
-        for h in (1, 2, 0, 3):
-            nc.sync.dma_start(out=og_raw[h][:], in_=og[h].rearrange("(u m c) e -> m u (c e)", u=2, c=2))
+        load_og(0)
+        load_og(3)
 
-        def cast_k(a):
+        def cast_k(a, lo, hi):
             nc.vector.tensor_copy(
-                out=k_bf[:, :, a * ROWS : (a + 1) * ROWS, :].rearrange("p r s j -> p s j r"),
-                in_=k_raw[a][:].rearrange("p j (s r) -> p s j r", r=PACK),
+                out=k_bf[:, lo:hi, a * ROWS : (a + 1) * ROWS, :],
+                in_=k_raw[a][:].rearrange("p j (s r) -> p r s j", r=PACK)[:, lo:hi],
             )
 
-        def cast_q(n, copy, lo, hi):
-            raw = qa_raw[n][:] if n < 2 else qb_raw[:, :, (n - 2) * HALF : (n - 1) * HALF]
-            copy(
-                out=q_bf[n][:].rearrange("p c (a b) j -> p a j b c", b=2)[:, lo:hi],
-                in_=raw.rearrange("p j (a b c) -> p a j b c", b=2, c=2)[:, lo:hi],
+        def quant_k(r):
+            nc.vector.quantize_mx(
+                out=k_codes[:, r * P : (r + 1) * P].bitcast(FP8X4),
+                scales=k_scales[:, r * P : (r + 1) * P],
+                in_=k_bf[:, r].rearrange("p s j -> p (s j)"),
             )
+
+        def cast_q(n):
+            raw = qa_raw[n][:] if n < 2 else qb_raw[:, :, (n - 2) * HALF : (n - 1) * HALF]
+            nc.vector.tensor_copy(out=q_bf[n][:], in_=raw.rearrange("p j q -> p q j"))
 
         def quantize(codes, scales, grouped):
             nc.vector.quantize_mx(out=codes[:].bitcast(FP8X4), scales=scales[:], in_=grouped)
 
         def quant_q(n):
-            quantize(q_codes[n], q_scales[n], q_bf[n][:].rearrange("p c m j -> p (c m j)"))
+            quantize(q_codes[n], q_scales[n], q_bf[n][:].rearrange("p q j -> p (q j)"))
 
-        def cast_v(g):
+        def cast_v():
             nc.vector.tensor_tensor(
-                out=v_bf[:, g].rearrange("p (a b) j -> p a j b", b=PACK),
-                in0=v_raw[:, g].rearrange("p j (a b) -> p a j b", b=PACK),
-                in1=sign[:].bitcast(F32).to_broadcast([P, E // PACK, PACK, PACK]),
+                out=v_bf[:],
+                in0=v_raw[:].rearrange("p g j e -> p g e j"),
+                in1=sign[:].bitcast(F32).to_broadcast([P, KV, E, PACK]),
                 op=ALU.mult,
             )
 
-        def scores(i):
-            pair, half, g = UNITS[i]
-            n = 2 * pair + half
+        def score_mm(n, g, r, c, dst):
             rows = slice(g * ROWS, (g + 1) * ROWS)
-            for r in range(PACK):
-                for c in range(2):
-                    tok = slice(r * P, (r + 1) * P)
-                    qs = slice(c * P, (c + 1) * P)
-                    nc.tensor.matmul_mx(
-                        out=score[g][r // 2][:, r % 2, qs],
-                        lhsT=k_codes[rows, tok].bitcast(FP8X4),
-                        lhsT_scale=k_scales[rows, tok],
-                        rhs=q_codes[n][rows, qs].bitcast(FP8X4),
-                        rhs_scale=q_scales[n][rows, qs],
-                        start=True,
-                        stop=True,
-                    )
+            tok = slice(r * P, (r + 1) * P)
+            qs = slice(c * P, (c + 1) * P)
+            nc.tensor.matmul_mx(
+                out=dst[:, qs],
+                lhsT=k_codes[rows, tok].bitcast(FP8X4),
+                lhsT_scale=k_scales[rows, tok],
+                rhs=q_codes[n][rows, qs].bitcast(FP8X4),
+                rhs_scale=q_scales[n][rows, qs],
+                start=True,
+                stop=True,
+            )
 
-        def weights(i):
-            g = UNITS[i][2]
-            for r in range(PACK):
-                nc.scalar.activation(
-                    out=w_rows[i][:, r, :], in_=score[g][r // 2][:, r % 2, :], func=ACT.Exp, bias=bias[:, r : r + 1]
-                )
+        def place(n, g, r):
+            if n < 3:
+                return score[g][r % 2][:, 0, :]
+            return score[g][r // 2][:, r % 2, :]
+
+        def scores(n, r):
+            for c in range(2):
+                for g in range(2):
+                    score_mm(n, g, r, c, place(n, g, r))
+
+        def weight(n, g, r):
+            nc.scalar.activation(
+                out=w_rows[2 * n + g][:, r, :].rearrange("p (c m) -> p c m", c=2),
+                in_=place(n, g, r).rearrange("p (m c) -> p c m", c=2),
+                func=ACT.Exp,
+                bias=bias[:, r : r + 1],
+            )
+
+        def weights(n, r):
+            for g in range(2):
+                weight(n, g, r)
 
         def group_w(i):
-            nc.vector.tensor_copy(
-                out=w_bf[i][:].rearrange("p (a b) r -> p a r b", b=PACK),
-                in_=w_rows[i][:].rearrange("p r (a b) -> p a r b", b=PACK),
-            )
+            nc.vector.tensor_copy(out=w_bf[i][:], in_=w_rows[i][:].rearrange("p r q -> p q r"))
 
         def quant_w(i):
             quantize(w_codes[i], w_scales[i], w_bf[i][:].rearrange("p q r -> p (q r)"))
+
+        def y_of(i):
+            return y[0][:, 1] if i == 7 else y[i // 2][:, i % 2]
 
         def values(i):
             g = UNITS[i][2]
@@ -172,7 +192,7 @@ def tile_rows_a_exp_kb_sink_gate_kernel(tc, qT, kT, t, v, kb, sink, og, out):
             for c in range(2):
                 qs = slice(c * P, (c + 1) * P)
                 nc.tensor.matmul_mx(
-                    out=y[i % 4][:, c, :],
+                    out=y_of(i)[:, c, :],
                     lhsT=w_codes[i][:, qs].bitcast(FP8X4),
                     lhsT_scale=w_scales[i][:, qs],
                     rhs=v_codes[:, feats].bitcast(FP8X4),
@@ -181,40 +201,49 @@ def tile_rows_a_exp_kb_sink_gate_kernel(tc, qT, kT, t, v, kb, sink, og, out):
                     stop=True,
                 )
 
-        def gate_tanh(i):
-            nc.scalar.activation(out=tanh[i][:], in_=og_raw[head_of(i)][:, UNITS[i][1], :], func=ACT.Tanh, scale=0.5)
+        def gates(h, lo, hi):
+            nc.scalar.activation(out=tanh[h][:, lo:hi], in_=og_raw[h][:, lo:hi], func=ACT.Tanh, scale=0.5)
 
-        def gate_vector(i):
-            nc.vector.tensor_scalar(
-                out=gate[i][:], in0=tanh[i][:], scalar1=0.5, scalar2=0.5, op0=ALU.mult, op1=ALU.add
+        def gates_affine(h, lo, hi):
+            nc.scalar.activation(out=gate[h][:, lo:hi], in_=tanh[h][:, lo:hi], func=ACT.Copy, scale=0.5, bias=0.5)
+
+        def denominators(n):
+            first, last = PAIRS[n // 2]
+            nc.vector.tensor_tensor(
+                out=den[n][:],
+                in0=y[n][:, :, :, E - 1],
+                in1=sink_raw[:, first : last + 1 : last - first, n % 2, :],
+                op=ALU.add,
             )
-
-        def gate_scalar(i):
-            nc.scalar.activation(out=gate[i][:], in_=tanh[i][:], func=ACT.Copy, scale=0.5, bias=0.5)
 
         def denominator(i):
             nc.vector.tensor_tensor(
-                out=den[i][:], in0=y[i % 4][:, 0:2, E - 1], in1=sink_raw[:, head_of(i), UNITS[i][1], :], op=ALU.add
+                out=den[i - 3][:, i % 2], in0=y_of(i)[:, :, E - 1], in1=sink_raw[:, head_of(i), 1, :], op=ALU.add
             )
 
-        def invert(i):
-            nc.vector.reciprocal(out=rden[i][:], in_=den[i][:])
+        def invert(n):
+            nc.vector.reciprocal(out=rden[n][:], in_=den[n][:])
 
-        def finish(i):
-            for c in range(2):
+        def invert_one(i):
+            nc.vector.reciprocal(out=rden[i - 3][:, i % 2], in_=den[i - 3][:, i % 2])
+
+        def finish(i, parts=(0, 1)):
+            slot = i - 3 if i >= 6 else i // 2
+            for c in parts:
                 nc.vector.scalar_tensor_tensor(
                     out=res[i][:, c, :],
-                    in0=y[i % 4][:, c, :],
-                    scalar=rden[i][:, c : c + 1],
-                    in1=gate[i][:, c * E : (c + 1) * E],
+                    in0=y_of(i)[:, c, :],
+                    scalar=rden[slot][:, i % 2, c : c + 1],
+                    in1=gate[head_of(i)][:, UNITS[i][1], c * E : (c + 1) * E],
                     op0=ALU.mult,
                     op1=ALU.mult,
                 )
             half = UNITS[i][1]
-            nc.sync.dma_start(
-                out=out[head_of(i), half * HALF : (half + 1) * HALF, :].rearrange("(m c) e -> m c e", c=2),
-                in_=res[i][:],
-            )
+            if 1 in parts:
+                nc.sync.dma_start(
+                    out=out[head_of(i), half * HALF : (half + 1) * HALF, :].rearrange("(m c) e -> m c e", c=2),
+                    in_=res[i][:],
+                )
 
         nc.gpsimd.memset(warm_in[:], 1.0)
         nc.scalar.activation(out=warm_out[0][:], in_=warm_in[:], func=ACT.Ln)
@@ -226,78 +255,116 @@ def tile_rows_a_exp_kb_sink_gate_kernel(tc, qT, kT, t, v, kb, sink, og, out):
             out=expo[:], in0=t_bits, scalar1=23, scalar2=0xFF, op0=ALU.logical_shift_right, op1=ALU.bitwise_and
         )
         nc.vector.tensor_scalar(
-            out=sign[:, 0, :, 0], in0=t_bits, scalar1=SIGN_BIT, scalar2=ONE_BITS, op0=ALU.bitwise_and, op1=ALU.bitwise_or
+            out=sign[:, 0, 0, :], in0=t_bits, scalar1=SIGN_BIT, scalar2=ONE_BITS, op0=ALU.bitwise_and, op1=ALU.bitwise_or
         )
         nc.scalar.activation(out=mant_ln[:], in_=mant[:].bitcast(F32), func=ACT.Ln)
         nc.scalar.activation(out=warm_out[1][:], in_=warm_in[:], func=ACT.Exp)
         nc.vector.tensor_scalar(
             out=expo_ln[:], in0=expo[:], scalar1=-127.0, scalar2=math.log(2.0), op0=ALU.add, op1=ALU.mult
         )
-        cast_k(0)
+        cast_q(0)
         nc.vector.tensor_tensor(out=bias_part[:], in0=expo_ln[:], in1=kb_raw[:], op=ALU.add)
-        cast_k(1)
-        nc.vector.tensor_tensor(out=bias[:], in0=bias_part[:], in1=mant_ln[:], op=ALU.add)
-        quantize(k_codes, k_scales, k_bf[:].rearrange("p r s j -> p (r s j)"))
-        cast_q(0, nc.vector.tensor_copy, 0, V_SHARE)
-        cast_q(0, nc.scalar.copy, V_SHARE, 64)
         quant_q(0)
-        scores(0)
-        scores(1)
-        cast_q(1, nc.scalar.copy, V_SHARE, 64)
-        cast_q(1, nc.vector.tensor_copy, 0, V_SHARE)
-        weights(0)
+        cast_k(0, 0, PACK)
+        nc.vector.tensor_tensor(out=bias[:], in0=bias_part[:], in1=mant_ln[:], op=ALU.add)
+        cast_k(1, 0, 1)
+        cast_k(1, 1, 2)
+        quant_k(0)
+        scores(0, 0)
+        cast_k(1, 2, 3)
+        quant_k(1)
+        scores(0, 1)
+        cast_k(1, 3, 4)
+        quant_k(2)
+        cast_q(1)
+        quant_k(3)
+        weights(0, 0)
         nc.scalar.dma_start(out=qb_raw[ROWS:P], in_=qT[3].rearrange("(p j) n -> p j n", j=PACK))
-        cast_v(0)
+        scores(0, 2)
+        weights(0, 1)
+        scores(0, 3)
         quant_q(1)
-        scores(2)
-        cast_v(1)
-        weights(1)
-        scores(3)
+        weights(0, 2)
+        scores(1, 0)
+        weights(0, 3)
+        scores(1, 1)
+        cast_v()
         group_w(0)
         quantize(v_codes, v_scales, v_bf[:].rearrange("p g e j -> p (g e j)"))
+        cast_q(2)
         quant_w(0)
-        values(0)
-        cast_q(2, nc.vector.tensor_copy, 0, 64)
         group_w(1)
         quant_q(2)
-        weights(2)
-        scores(4)
+        weights(1, 0)
+        scores(1, 2)
+        weights(1, 1)
+        scores(1, 3)
+        values(0)
         quant_w(1)
+        weights(1, 2)
+        scores(2, 0)
+        weights(1, 3)
+        scores(2, 1)
         values(1)
-        weights(3)
-        scores(5)
+        gates(1, 0, 2)
+        gates(2, 0, 2)
+        gates_affine(1, 0, 2)
+        gates_affine(2, 0, 2)
         group_w(2)
-        cast_q(3, nc.vector.tensor_copy, 0, 64)
+        cast_q(3)
         quant_w(2)
         values(2)
+        group_w(3)
         quant_q(3)
-        gate_tanh(0)
-        gate_tanh(1)
-        for i in range(3, 8):
-            if i + 1 < 8:
-                weights(i + 1)
-                if i + 3 < 8:
-                    scores(i + 3)
-                gate_tanh(i - 1)
-            if i == 7:
-                gate_tanh(6)
-                gate_tanh(7)
-                gate_scalar(6)
-                gate_scalar(7)
-            denominator(i - 3)
-            group_w(i)
-            invert(i - 3)
-            gate_vector(i - 3)
-            quant_w(i)
-            finish(i - 3)
-            values(i)
-        denominator(5)
+        denominators(0)
+        quant_w(3)
+        invert(0)
+        weights(2, 0)
+        scores(2, 2)
+        values(3)
+        weights(2, 1)
+        scores(2, 3)
+        denominators(1)
+        finish(0)
+        invert(1)
+        finish(1)
+        weights(2, 2)
+        weights(2, 3)
+        for r in range(PACK):
+            scores(3, r)
+        finish(2)
+        group_w(4)
+        finish(3)
+        group_w(5)
+        quant_w(4)
+        values(4)
+        gates(0, 0, 1)
+        gates(3, 0, 1)
+        gates_affine(0, 0, 1)
+        gates_affine(3, 0, 1)
+        quant_w(5)
+        values(5)
+        for g in range(2):
+            for r in range(PACK):
+                weight(3, g, r)
+        gates(0, 1, 2)
+        gates(3, 1, 2)
+        gates_affine(0, 1, 2)
+        gates_affine(3, 1, 2)
+        denominators(2)
+        group_w(6)
+        invert(2)
+        quant_w(6)
+        values(6)
+        finish(4)
+        group_w(7)
         denominator(6)
-        gate_vector(5)
-        invert(5)
-        invert(6)
-        denominator(7)
+        quant_w(7)
+        values(7)
+        invert_one(6)
         finish(5)
-        invert(7)
-        finish(6)
+        denominator(7)
+        finish(6, (0,))
+        invert_one(7)
+        finish(6, (1,))
         finish(7)

@@ -19,6 +19,7 @@ P = 128
 ROWS = 64
 PACK = 4
 HALF = 256
+QUAD = 32
 ONE_BITS = 0x3F800000
 MANTISSA = 0x007FFFFF
 SIGN_BIT = -0x80000000
@@ -42,7 +43,9 @@ def tile_rows_a_exp_kb_sink_gate_kernel(tc, qT, kT, t, v, kb, sink, og, out):
 
         t_raw = tile("t_raw", [P, PACK], F32)
         kb_raw = tile("kb_raw", [P, PACK], F32)
-        sink_raw = tile("sink_raw", [P, H, 2, 2], F32)
+        sink_rows = tile("sink_rows", [P, 2, 2 * QUAD], F32)
+        sink_dealt = tile("sink_dealt", [P, 2, 2, QUAD], F32)
+        sink_cols = tile("sink_cols", [P, 2, 2, QUAD], F32)
         mant = tile("mant", [P, PACK], I32)
         expo = tile("expo", [P, PACK], I32)
         sign = tile("sign", [P, 1, 1, PACK], I32)
@@ -58,7 +61,7 @@ def tile_rows_a_exp_kb_sink_gate_kernel(tc, qT, kT, t, v, kb, sink, og, out):
         k_codes = tile("k_codes", [P, N], U32)
         k_scales = tile("k_scales", [P, N], U8)
         qa_raw = tiles("qa_raw", 2, [P, PACK, HALF], F32)
-        qb_raw = tile("qb_raw", [P, PACK, NQ], F32)
+        qb_raw = tiles("qb_raw", 2, [P, PACK, HALF], F32)
         q_bf = tiles("q_bf", 4, [P, HALF, PACK], BF16)
         q_codes = tiles("q_codes", 4, [P, HALF], U32)
         q_scales = tiles("q_scales", 4, [P, HALF], U8)
@@ -66,13 +69,13 @@ def tile_rows_a_exp_kb_sink_gate_kernel(tc, qT, kT, t, v, kb, sink, og, out):
         v_bf = tile("v_bf", [P, KV, E, PACK], BF16)
         v_codes = tile("v_codes", [P, KV * E], U32)
         v_scales = tile("v_scales", [P, KV * E], U8)
-        og_raw = tiles("og_raw", H, [P, 2, 2 * E], F32)
+        og_raw = tile("og_raw", [P, H, 2, 2 * E], F32)
         w_rows = tiles("w_rows", 8, [P, PACK, HALF], BF16)
         w_bf = tiles("w_bf", 8, [P, HALF, PACK], BF16)
         w_codes = tiles("w_codes", 8, [P, HALF], U32)
         w_scales = tiles("w_scales", 8, [P, HALF], U8)
-        tanh = tiles("tanh", H, [P, 2, 2 * E], F32)
-        gate = tiles("gate", H, [P, 2, 2 * E], F32)
+        tanh = tile("tanh", [P, H, 2, 2 * E], F32)
+        gate = tile("gate", [P, H, 2, 2 * E], F32)
         den = tiles("den", 5, [P, 2, 2], F32)
         rden = tiles("rden", 5, [P, 2, 2], F32)
         res = tiles("res", 8, [P, 2, E], F32)
@@ -84,6 +87,8 @@ def tile_rows_a_exp_kb_sink_gate_kernel(tc, qT, kT, t, v, kb, sink, og, out):
             pair, half, g = UNITS[i]
             return PAIRS[pair][g]
 
+        nc.gpsimd.memset(warm_in[:], 1.0)
+        nc.gpsimd.memset(sink_rows[:], 0.0)
         nc.scalar.dma_start(out=t_raw[:], in_=t.rearrange("(p j) o -> p (j o)", j=PACK))
         nc.scalar.dma_start(out=kb_raw[:], in_=kb.rearrange("(p j) o -> p (j o)", j=PACK))
         k_view = kT.rearrange("g (p j) n -> (g p) j n", j=PACK)
@@ -96,22 +101,35 @@ def tile_rows_a_exp_kb_sink_gate_kernel(tc, qT, kT, t, v, kb, sink, og, out):
             out=v_raw[:].rearrange("p g j e -> p g (j e)"),
             in_=v.rearrange("g (p j) e -> p g (j e)", j=PACK),
         )
-        nc.sync.dma_start(out=qb_raw[0:ROWS], in_=qT[0].rearrange("(p j) n -> p j n", j=PACK))
+        for h in range(H):
+            nc.sync.dma_start(
+                out=sink_rows[h:P:QUAD], in_=sink[h].rearrange("(u a n) o -> a u (n o)", u=2, n=2 * QUAD)
+            )
+
+        def load_qb(a):
+            for g in range(2):
+                nc.sync.dma_start(
+                    out=qb_raw[a][g * ROWS : (g + 1) * ROWS],
+                    in_=qT[PAIRS[1][g]].rearrange("(p j) n -> p j n", j=PACK)[:, :, a * HALF : (a + 1) * HALF],
+                )
 
         def load_og(h):
-            nc.sync.dma_start(out=og_raw[h][:], in_=og[h].rearrange("(u m c) e -> m u (c e)", u=2, c=2))
+            nc.sync.dma_start(out=og_raw[:, h], in_=og[h].rearrange("(u m c) e -> m u (c e)", u=2, c=2))
 
+        load_qb(0)
         load_og(1)
         load_og(2)
-        nc.sync.dma_start(
-            out=sink_raw[:].rearrange("p h u c -> p (h u) c"),
-            in_=sink.rearrange("h (u m c) o -> m (h u) (c o)", u=2, c=2),
-        )
+        load_qb(1)
         load_og(0)
         load_og(3)
 
-        def cast_k(a, lo, hi):
-            nc.vector.tensor_copy(
+        def turn_sink():
+            nc.vector.transpose(
+                out=sink_cols[:].rearrange("p u c h -> p (u c h)"), in_=sink_dealt[:].rearrange("p u c n -> p (u c n)")
+            )
+
+        def cast_k(a, lo, hi, copy=nc.vector.tensor_copy):
+            copy(
                 out=k_bf[:, lo:hi, a * ROWS : (a + 1) * ROWS, :],
                 in_=k_raw[a][:].rearrange("p j (s r) -> p r s j", r=PACK)[:, lo:hi],
             )
@@ -123,9 +141,9 @@ def tile_rows_a_exp_kb_sink_gate_kernel(tc, qT, kT, t, v, kb, sink, og, out):
                 in_=k_bf[:, r].rearrange("p s j -> p (s j)"),
             )
 
-        def cast_q(n):
-            raw = qa_raw[n][:] if n < 2 else qb_raw[:, :, (n - 2) * HALF : (n - 1) * HALF]
-            nc.vector.tensor_copy(out=q_bf[n][:], in_=raw.rearrange("p j q -> p q j"))
+        def cast_q(n, lo=0, hi=HALF, copy=nc.vector.tensor_copy):
+            raw = qa_raw[n] if n < 2 else qb_raw[n - 2]
+            copy(out=q_bf[n][:, lo:hi], in_=raw[:].rearrange("p j q -> p q j")[:, lo:hi])
 
         def quantize(codes, scales, grouped):
             nc.vector.quantize_mx(out=codes[:].bitcast(FP8X4), scales=scales[:], in_=grouped)
@@ -177,8 +195,8 @@ def tile_rows_a_exp_kb_sink_gate_kernel(tc, qT, kT, t, v, kb, sink, og, out):
             for g in range(2):
                 weight(n, g, r)
 
-        def group_w(i):
-            nc.vector.tensor_copy(out=w_bf[i][:], in_=w_rows[i][:].rearrange("p r q -> p q r"))
+        def group_w(i, lo=0, hi=HALF, copy=nc.vector.tensor_copy):
+            copy(out=w_bf[i][:, lo:hi], in_=w_rows[i][:].rearrange("p r q -> p q r")[:, lo:hi])
 
         def quant_w(i):
             quantize(w_codes[i], w_scales[i], w_bf[i][:].rearrange("p q r -> p (q r)"))
@@ -201,24 +219,28 @@ def tile_rows_a_exp_kb_sink_gate_kernel(tc, qT, kT, t, v, kb, sink, og, out):
                     stop=True,
                 )
 
-        def gates(h, lo, hi):
-            nc.scalar.activation(out=tanh[h][:, lo:hi], in_=og_raw[h][:, lo:hi], func=ACT.Tanh, scale=0.5)
+        def heads(pair):
+            first, last = PAIRS[pair]
+            return slice(first, last + 1, last - first)
 
-        def gates_affine(h, lo, hi):
-            nc.scalar.activation(out=gate[h][:, lo:hi], in_=tanh[h][:, lo:hi], func=ACT.Copy, scale=0.5, bias=0.5)
+        def tanhs(hs, us):
+            nc.scalar.activation(out=tanh[:, hs, us], in_=og_raw[:, hs, us], func=ACT.Tanh, scale=0.5)
+
+        def gates(hs, us):
+            nc.scalar.activation(out=gate[:, hs, us], in_=tanh[:, hs, us], func=ACT.Copy, scale=0.5, bias=0.5)
 
         def denominators(n):
             first, last = PAIRS[n // 2]
             nc.vector.tensor_tensor(
                 out=den[n][:],
                 in0=y[n][:, :, :, E - 1],
-                in1=sink_raw[:, first : last + 1 : last - first, n % 2, :],
+                in1=sink_cols[:, n % 2, :, first : last + 1 : last - first].rearrange("p c g -> p g c"),
                 op=ALU.add,
             )
 
         def denominator(i):
             nc.vector.tensor_tensor(
-                out=den[i - 3][:, i % 2], in0=y_of(i)[:, :, E - 1], in1=sink_raw[:, head_of(i), 1, :], op=ALU.add
+                out=den[i - 3][:, i % 2], in0=y_of(i)[:, :, E - 1], in1=sink_cols[:, 1, :, head_of(i)], op=ALU.add
             )
 
         def invert(n):
@@ -234,7 +256,7 @@ def tile_rows_a_exp_kb_sink_gate_kernel(tc, qT, kT, t, v, kb, sink, og, out):
                     out=res[i][:, c, :],
                     in0=y_of(i)[:, c, :],
                     scalar=rden[slot][:, i % 2, c : c + 1],
-                    in1=gate[head_of(i)][:, UNITS[i][1], c * E : (c + 1) * E],
+                    in1=gate[:, head_of(i), UNITS[i][1], c * E : (c + 1) * E],
                     op0=ALU.mult,
                     op1=ALU.mult,
                 )
@@ -245,28 +267,20 @@ def tile_rows_a_exp_kb_sink_gate_kernel(tc, qT, kT, t, v, kb, sink, og, out):
                     in_=res[i][:],
                 )
 
-        nc.gpsimd.memset(warm_in[:], 1.0)
         nc.scalar.activation(out=warm_out[0][:], in_=warm_in[:], func=ACT.Ln)
-        t_bits = t_raw[:].bitcast(I32)
-        nc.vector.tensor_scalar(
-            out=mant[:], in0=t_bits, scalar1=MANTISSA, scalar2=ONE_BITS, op0=ALU.bitwise_and, op1=ALU.bitwise_or
-        )
-        nc.vector.tensor_scalar(
-            out=expo[:], in0=t_bits, scalar1=23, scalar2=0xFF, op0=ALU.logical_shift_right, op1=ALU.bitwise_and
-        )
-        nc.vector.tensor_scalar(
-            out=sign[:, 0, 0, :], in0=t_bits, scalar1=SIGN_BIT, scalar2=ONE_BITS, op0=ALU.bitwise_and, op1=ALU.bitwise_or
-        )
+        nc.vector.tensor_scalar(out=mant[:], in0=t_raw[:].bitcast(I32), scalar1=MANTISSA, scalar2=ONE_BITS, op0=ALU.bitwise_and, op1=ALU.bitwise_or)
+        nc.vector.tensor_scalar(out=expo[:], in0=t_raw[:].bitcast(I32), scalar1=23, scalar2=0xFF, op0=ALU.logical_shift_right, op1=ALU.bitwise_and)
+        nc.vector.tensor_scalar(out=sign[:, 0, 0, :], in0=t_raw[:].bitcast(I32), scalar1=SIGN_BIT, scalar2=ONE_BITS, op0=ALU.bitwise_and, op1=ALU.bitwise_or)
         nc.scalar.activation(out=mant_ln[:], in_=mant[:].bitcast(F32), func=ACT.Ln)
         nc.scalar.activation(out=warm_out[1][:], in_=warm_in[:], func=ACT.Exp)
-        nc.vector.tensor_scalar(
-            out=expo_ln[:], in0=expo[:], scalar1=-127.0, scalar2=math.log(2.0), op0=ALU.add, op1=ALU.mult
-        )
+        nc.vector.tensor_scalar(out=expo_ln[:], in0=expo[:], scalar1=-127.0, scalar2=math.log(2.0), op0=ALU.add, op1=ALU.mult)
         cast_q(0)
         nc.vector.tensor_tensor(out=bias_part[:], in0=expo_ln[:], in1=kb_raw[:], op=ALU.add)
         quant_q(0)
-        cast_k(0, 0, PACK)
         nc.vector.tensor_tensor(out=bias[:], in0=bias_part[:], in1=mant_ln[:], op=ALU.add)
+        cast_k(0, 3, 4, nc.scalar.copy)
+        cast_k(0, 0, 3)
+        cast_k(1, 3, 4, nc.scalar.copy)
         cast_k(1, 0, 1)
         cast_k(1, 1, 2)
         quant_k(0)
@@ -274,97 +288,92 @@ def tile_rows_a_exp_kb_sink_gate_kernel(tc, qT, kT, t, v, kb, sink, og, out):
         cast_k(1, 2, 3)
         quant_k(1)
         scores(0, 1)
-        cast_k(1, 3, 4)
-        quant_k(2)
         cast_q(1)
+        quant_k(2)
         quant_k(3)
+        quant_q(1)
         weights(0, 0)
-        nc.scalar.dma_start(out=qb_raw[ROWS:P], in_=qT[3].rearrange("(p j) n -> p j n", j=PACK))
         scores(0, 2)
         weights(0, 1)
         scores(0, 3)
-        quant_q(1)
         weights(0, 2)
         scores(1, 0)
         weights(0, 3)
         scores(1, 1)
         cast_v()
+        nc.vector.tensor_copy(out=sink_dealt[:], in_=sink_rows[:].rearrange("p u (n c) -> p u c n", c=2))
         group_w(0)
         quantize(v_codes, v_scales, v_bf[:].rearrange("p g e j -> p (g e j)"))
         cast_q(2)
         quant_w(0)
         group_w(1)
         quant_q(2)
+        turn_sink()
+        quant_w(1)
         weights(1, 0)
         scores(1, 2)
         weights(1, 1)
         scores(1, 3)
-        values(0)
-        quant_w(1)
         weights(1, 2)
-        scores(2, 0)
         weights(1, 3)
+        scores(2, 0)
         scores(2, 1)
+        values(0)
         values(1)
-        gates(1, 0, 2)
-        gates(2, 0, 2)
-        gates_affine(1, 0, 2)
-        gates_affine(2, 0, 2)
+        tanhs(heads(0), slice(0, 2))
         group_w(2)
         cast_q(3)
         quant_w(2)
-        values(2)
-        group_w(3)
-        quant_q(3)
         denominators(0)
-        quant_w(3)
+        quant_q(3)
+        group_w(3)
         invert(0)
+        quant_w(3)
         weights(2, 0)
         scores(2, 2)
-        values(3)
         weights(2, 1)
         scores(2, 3)
-        denominators(1)
-        finish(0)
-        invert(1)
-        finish(1)
+        values(2)
         weights(2, 2)
         weights(2, 3)
-        for r in range(PACK):
-            scores(3, r)
-        finish(2)
+        scores(3, 0)
+        scores(3, 1)
+        values(3)
+        scores(3, 2)
+        scores(3, 3)
+        gates(heads(0), slice(0, 2))
+        tanhs(heads(1), 0)
         group_w(4)
-        finish(3)
         group_w(5)
         quant_w(4)
         values(4)
-        gates(0, 0, 1)
-        gates(3, 0, 1)
-        gates_affine(0, 0, 1)
-        gates_affine(3, 0, 1)
+        denominators(1)
         quant_w(5)
         values(5)
+        invert(1)
+        finish(0)
+        finish(1)
+        finish(2)
         for g in range(2):
-            for r in range(PACK):
-                weight(3, g, r)
-        gates(0, 1, 2)
-        gates(3, 1, 2)
-        gates_affine(0, 1, 2)
-        gates_affine(3, 1, 2)
-        denominators(2)
+            for r in range(PACK): weight(3, g, r)
+        gates(heads(1), 0)
+        group_w(7, 128, 256, nc.scalar.copy)
+        tanhs(heads(1), 1)
+        gates(heads(1), 1)
         group_w(6)
-        invert(2)
+        denominators(2)
+        finish(3)
         quant_w(6)
         values(6)
-        finish(4)
-        group_w(7)
-        denominator(6)
+        group_w(7, 0, 128)
+        invert(2)
         quant_w(7)
         values(7)
+        denominator(6)
+        finish(4)
         invert_one(6)
-        finish(5)
         denominator(7)
-        finish(6, (0,))
+        finish(5)
         invert_one(7)
-        finish(6, (1,))
+        finish(6)
         finish(7)

@@ -18,14 +18,19 @@ ACT = mybir.ActivationFunctionType
 P = 128
 ROWS = 64
 PACK = 4
-HALF = 256
+HALF = NQ // 2
 QUAD = 32
-ONE_BITS = 0x3F800000
-MANTISSA = 0x007FFFFF
-SIGN_BIT = -0x80000000
 
-PAIRS = ((1, 2), (0, 3))
-UNITS = [(pair, half, g) for pair in range(2) for half in range(2) for g in range(2)]
+MANTISSA_MASK = 0x007FFFFF
+SIGN_MASK = -0x80000000
+ONE_BITS = 0x3F800000
+EXPONENT_SHIFT, EXPONENT_MASK, EXPONENT_BIAS = 23, 0xFF, 127.0
+
+UNITS = [(0, 0), (3, 0), (0, 1), (3, 1), (1, 0), (2, 0), (1, 1), (2, 1)]
+GROUPS = [(0, 1), (2, 3), (4, 5), (6,), (7,)]
+GROUP_OF = {unit: n for n, group in enumerate(GROUPS) for unit in group}
+Y_BANKS = 4
+TURN_ABOUT = (0, 4, 5)
 
 
 def tile_rows_a_exp_kb_sink_gate_kernel(tc, qT, kT, t, v, kb, sink, og, out):
@@ -39,29 +44,28 @@ def tile_rows_a_exp_kb_sink_gate_kernel(tc, qT, kT, t, v, kb, sink, og, out):
             return sb.tile(shape, dtype, name=name, align_bytes=64)
 
         def tiles(name, count, shape, dtype):
-            return [tile("%s%d" % (name, i), shape, dtype) for i in range(count)]
+            return [tile("%s%d" % (name, n), shape, dtype) for n in range(count)]
 
         t_raw = tile("t_raw", [P, PACK], F32)
         kb_raw = tile("kb_raw", [P, PACK], F32)
-        sink_rows = tile("sink_rows", [P, 2, 2 * QUAD], F32)
-        sink_dealt = tile("sink_dealt", [P, 2, 2, QUAD], F32)
-        sink_cols = tile("sink_cols", [P, 2, 2, QUAD], F32)
-        mant = tile("mant", [P, PACK], I32)
-        expo = tile("expo", [P, PACK], I32)
+        mantissa = tile("mantissa", [P, PACK], I32)
+        exponent = tile("exponent", [P, PACK], I32)
         sign = tile("sign", [P, 1, 1, PACK], I32)
-        expo_ln = tile("expo_ln", [P, PACK], F32)
+        ln_power = tile("ln_power", [P, PACK], F32)
+        ln_mantissa = tile("ln_mantissa", [P, PACK], F32)
         bias_part = tile("bias_part", [P, PACK], F32)
-        mant_ln = tile("mant_ln", [P, PACK], F32)
         bias = tile("bias", [P, PACK], F32)
         warm_in = tile("warm_in", [P, 1], F32)
         warm_out = tiles("warm_out", 2, [P, 1], F32)
 
-        k_raw = tiles("k_raw", 2, [P, PACK, HALF], F32)
+        sink_rows = tile("sink_rows", [P, 2, 2 * QUAD], F32)
+        sink_dealt = tile("sink_dealt", [P, 2, 2, QUAD], F32)
+        sink_cols = tile("sink_cols", [P, 2, 2, QUAD], F32)
+
+        k_raw = tile("k_raw", [P, PACK, N], F32)
         k_bf = tile("k_bf", [P, PACK, P, PACK], BF16)
-        k_codes = tile("k_codes", [P, N], U32)
-        k_scales = tile("k_scales", [P, N], U8)
-        qa_raw = tiles("qa_raw", 2, [P, PACK, HALF], F32)
-        qb_raw = tiles("qb_raw", 2, [P, PACK, HALF], F32)
+        k_mx = tiles("k_mx", 2, [P, N + N // PACK], I32)
+        q_raw = tiles("q_raw", 4, [P, PACK, HALF], F32)
         q_bf = tiles("q_bf", 4, [P, HALF, PACK], BF16)
         q_codes = tiles("q_codes", 4, [P, HALF], U32)
         q_scales = tiles("q_scales", 4, [P, HALF], U8)
@@ -70,310 +74,308 @@ def tile_rows_a_exp_kb_sink_gate_kernel(tc, qT, kT, t, v, kb, sink, og, out):
         v_codes = tile("v_codes", [P, KV * E], U32)
         v_scales = tile("v_scales", [P, KV * E], U8)
         og_raw = tile("og_raw", [P, H, 2, 2 * E], F32)
-        w_rows = tiles("w_rows", 8, [P, PACK, HALF], BF16)
-        w_bf = tiles("w_bf", 8, [P, HALF, PACK], BF16)
-        w_codes = tiles("w_codes", 8, [P, HALF], U32)
-        w_scales = tiles("w_scales", 8, [P, HALF], U8)
         tanh = tile("tanh", [P, H, 2, 2 * E], F32)
         gate = tile("gate", [P, H, 2, 2 * E], F32)
-        den = tiles("den", 5, [P, 2, 2], F32)
-        rden = tiles("rden", 5, [P, 2, 2], F32)
-        res = tiles("res", 8, [P, 2, E], F32)
+
+        w_rows = tiles("w_rows", len(UNITS), [P, PACK, HALF], BF16)
+        w_bf = tiles("w_bf", len(UNITS), [P, HALF, PACK], BF16)
+        w_codes = tiles("w_codes", len(UNITS), [P, HALF], U32)
+        w_scales = tiles("w_scales", len(UNITS), [P, HALF], U8)
+        den = tiles("den", len(GROUPS), [P, 2, 2], F32)
+        rden = tiles("rden", len(GROUPS), [P, 2, 2], F32)
+        res = tiles("res", len(UNITS), [P, 2, E], F32)
 
         score = [[ps.tile([P, 2, HALF], F32, name="score%d%d" % (g, b)) for b in range(2)] for g in range(2)]
-        y = [ps.tile([P, 2, 2, E], F32, name="y%d" % b) for b in range(4)]
+        y = [ps.tile([P, 2, 2, E], F32, name="y%d" % b) for b in range(Y_BANKS)]
 
-        def head_of(i):
-            pair, half, g = UNITS[i]
-            return PAIRS[pair][g]
-
-        nc.gpsimd.memset(warm_in[:], 1.0)
-        nc.gpsimd.memset(sink_rows[:], 0.0)
-        nc.scalar.dma_start(out=t_raw[:], in_=t.rearrange("(p j) o -> p (j o)", j=PACK))
-        nc.scalar.dma_start(out=kb_raw[:], in_=kb.rearrange("(p j) o -> p (j o)", j=PACK))
-        k_view = kT.rearrange("g (p j) n -> (g p) j n", j=PACK)
-        qa_view = qT[1:3].rearrange("g (p j) n -> (g p) j n", j=PACK)
-        nc.sync.dma_start(out=qa_raw[0][:], in_=qa_view[:, :, 0:HALF])
-        for a in range(2):
-            nc.sync.dma_start(out=k_raw[a][:], in_=k_view[:, :, a * HALF : (a + 1) * HALF])
-        nc.sync.dma_start(out=qa_raw[1][:], in_=qa_view[:, :, HALF:NQ])
-        nc.sync.dma_start(
-            out=v_raw[:].rearrange("p g j e -> p g (j e)"),
-            in_=v.rearrange("g (p j) e -> p g (j e)", j=PACK),
-        )
-        for h in range(H):
-            nc.sync.dma_start(
-                out=sink_rows[h:P:QUAD], in_=sink[h].rearrange("(u a n) o -> a u (n o)", u=2, n=2 * QUAD)
-            )
-
-        def load_qb(a):
-            for g in range(2):
-                nc.sync.dma_start(
-                    out=qb_raw[a][g * ROWS : (g + 1) * ROWS],
-                    in_=qT[PAIRS[1][g]].rearrange("(p j) n -> p j n", j=PACK)[:, :, a * HALF : (a + 1) * HALF],
-                )
+        def load_q(n):
+            two_heads = qT[2 * (n % 2) : 2 * (n % 2) + 2].rearrange("g (p j) q -> (g p) j q", j=PACK)
+            nc.sync.dma_start(out=q_raw[n][:], in_=two_heads[:, :, (n // 2) * HALF : (n // 2 + 1) * HALF])
 
         def load_og(h):
             nc.sync.dma_start(out=og_raw[:, h], in_=og[h].rearrange("(u m c) e -> m u (c e)", u=2, c=2))
 
-        load_qb(0)
-        load_og(1)
-        load_og(2)
-        load_qb(1)
-        load_og(0)
-        load_og(3)
-
-        def turn_sink():
-            nc.vector.transpose(
-                out=sink_cols[:].rearrange("p u c h -> p (u c h)"), in_=sink_dealt[:].rearrange("p u c n -> p (u c n)")
+        def load_sink(h):
+            nc.sync.dma_start(
+                out=sink_rows[h:P:QUAD], in_=sink[h].rearrange("(u a n) o -> a u (n o)", u=2, n=2 * QUAD)
             )
 
-        def cast_k(a, lo, hi, copy=nc.vector.tensor_copy):
-            copy(
-                out=k_bf[:, lo:hi, a * ROWS : (a + 1) * ROWS, :],
-                in_=k_raw[a][:].rearrange("p j (s r) -> p r s j", r=PACK)[:, lo:hi],
-            )
-
-        def quant_k(r):
-            nc.vector.quantize_mx(
-                out=k_codes[:, r * P : (r + 1) * P].bitcast(FP8X4),
-                scales=k_scales[:, r * P : (r + 1) * P],
-                in_=k_bf[:, r].rearrange("p s j -> p (s j)"),
-            )
-
-        def cast_q(n, lo=0, hi=HALF, copy=nc.vector.tensor_copy):
-            raw = qa_raw[n] if n < 2 else qb_raw[n - 2]
-            copy(out=q_bf[n][:, lo:hi], in_=raw[:].rearrange("p j q -> p q j")[:, lo:hi])
+        def swap_keys(g):
+            nc.sync.dma_start(out=k_mx[1][(1 - g) * ROWS : (2 - g) * ROWS], in_=k_mx[0][g * ROWS : (g + 1) * ROWS])
 
         def quantize(codes, scales, grouped):
-            nc.vector.quantize_mx(out=codes[:].bitcast(FP8X4), scales=scales[:], in_=grouped)
+            nc.vector.quantize_mx(out=codes.bitcast(FP8X4), scales=scales, in_=grouped)
+
+        def cast_k(r, copy):
+            copy(out=k_bf[:, r], in_=k_raw[:].rearrange("p j (s r) -> p r s j", r=PACK)[:, r])
+
+        def quant_k(r):
+            cols = slice(r * P, (r + 1) * P)
+            quantize(k_mx[0][:, cols], k_mx[0][:, N:].bitcast(U8)[:, cols], k_bf[:, r].rearrange("p s j -> p (s j)"))
+
+        def cast_q(n):
+            nc.vector.tensor_copy(out=q_bf[n][:], in_=q_raw[n][:].rearrange("p j q -> p q j"))
 
         def quant_q(n):
-            quantize(q_codes[n], q_scales[n], q_bf[n][:].rearrange("p q j -> p (q j)"))
+            quantize(q_codes[n][:], q_scales[n][:], q_bf[n][:].rearrange("p q j -> p (q j)"))
 
         def cast_v():
             nc.vector.tensor_tensor(
                 out=v_bf[:],
-                in0=v_raw[:].rearrange("p g j e -> p g e j"),
+                in0=v_raw[:].rearrange("p g r e -> p g e r"),
                 in1=sign[:].bitcast(F32).to_broadcast([P, KV, E, PACK]),
                 op=ALU.mult,
             )
 
-        def score_mm(n, g, r, c, dst):
-            rows = slice(g * ROWS, (g + 1) * ROWS)
-            tok = slice(r * P, (r + 1) * P)
-            qs = slice(c * P, (c + 1) * P)
+        def quant_v():
+            quantize(v_codes[:], v_scales[:], v_bf[:].rearrange("p g e r -> p (g e r)"))
+
+        def score_place(i, r):
+            banks = score[UNITS[i][0] % 2]
+            if i in TURN_ABOUT:
+                return banks[r % 2][:, r // 2, :]
+            return banks[r // 2][:, r % 2, :]
+
+        def score_matmul(i, r, part):
+            h, half = UNITS[i]
+            keys = k_mx[0 if h % 2 == h // 2 else 1]
+            n = 2 * half + h // 2
+            rows = slice(h % 2 * ROWS, (h % 2 + 1) * ROWS)
+            tokens = slice(r * P, (r + 1) * P)
+            queries = slice(part * P, (part + 1) * P)
             nc.tensor.matmul_mx(
-                out=dst[:, qs],
-                lhsT=k_codes[rows, tok].bitcast(FP8X4),
-                lhsT_scale=k_scales[rows, tok],
-                rhs=q_codes[n][rows, qs].bitcast(FP8X4),
-                rhs_scale=q_scales[n][rows, qs],
+                out=score_place(i, r)[:, queries],
+                lhsT=keys[rows, tokens].bitcast(FP8X4),
+                lhsT_scale=keys[rows, N:].bitcast(U8)[:, tokens],
+                rhs=q_codes[n][rows, queries].bitcast(FP8X4),
+                rhs_scale=q_scales[n][rows, queries],
                 start=True,
                 stop=True,
             )
 
-        def place(n, g, r):
-            if n < 3:
-                return score[g][r % 2][:, 0, :]
-            return score[g][r // 2][:, r % 2, :]
+        def scores(units, rs):
+            for r in rs:
+                for part in range(2):
+                    for i in units:
+                        score_matmul(i, r, part)
 
-        def scores(n, r):
-            for c in range(2):
-                for g in range(2):
-                    score_mm(n, g, r, c, place(n, g, r))
+        def weights(units, rs):
+            for r in rs:
+                for i in units:
+                    nc.scalar.activation(
+                        out=w_rows[i][:, r, :].rearrange("p (c m) -> p c m", c=2),
+                        in_=score_place(i, r).rearrange("p (m c) -> p c m", c=2),
+                        func=ACT.Exp,
+                        bias=bias[:, r : r + 1],
+                    )
 
-        def weight(n, g, r):
-            nc.scalar.activation(
-                out=w_rows[2 * n + g][:, r, :].rearrange("p (c m) -> p c m", c=2),
-                in_=place(n, g, r).rearrange("p (m c) -> p c m", c=2),
-                func=ACT.Exp,
-                bias=bias[:, r : r + 1],
-            )
-
-        def weights(n, r):
-            for g in range(2):
-                weight(n, g, r)
-
-        def group_w(i, lo=0, hi=HALF, copy=nc.vector.tensor_copy):
-            copy(out=w_bf[i][:, lo:hi], in_=w_rows[i][:].rearrange("p r q -> p q r")[:, lo:hi])
+        def group_w(i):
+            nc.vector.tensor_copy(out=w_bf[i][:], in_=w_rows[i][:].rearrange("p r q -> p q r"))
 
         def quant_w(i):
-            quantize(w_codes[i], w_scales[i], w_bf[i][:].rearrange("p q r -> p (q r)"))
+            quantize(w_codes[i][:], w_scales[i][:], w_bf[i][:].rearrange("p q r -> p (q r)"))
 
-        def y_of(i):
-            return y[0][:, 1] if i == 7 else y[i // 2][:, i % 2]
+        def y_place(i):
+            n = GROUP_OF[i]
+            return y[n % Y_BANKS][:, GROUPS[n].index(i)]
 
         def values(i):
-            g = UNITS[i][2]
-            feats = slice(g * E, (g + 1) * E)
+            features = slice(UNITS[i][0] // 2 * E, (UNITS[i][0] // 2 + 1) * E)
             for c in range(2):
-                qs = slice(c * P, (c + 1) * P)
+                queries = slice(c * P, (c + 1) * P)
                 nc.tensor.matmul_mx(
-                    out=y_of(i)[:, c, :],
-                    lhsT=w_codes[i][:, qs].bitcast(FP8X4),
-                    lhsT_scale=w_scales[i][:, qs],
-                    rhs=v_codes[:, feats].bitcast(FP8X4),
-                    rhs_scale=v_scales[:, feats],
+                    out=y_place(i)[:, c, :],
+                    lhsT=w_codes[i][:, queries].bitcast(FP8X4),
+                    lhsT_scale=w_scales[i][:, queries],
+                    rhs=v_codes[:, features].bitcast(FP8X4),
+                    rhs_scale=v_scales[:, features],
                     start=True,
                     stop=True,
                 )
 
-        def heads(pair):
-            first, last = PAIRS[pair]
-            return slice(first, last + 1, last - first)
+        def gate_tanh(heads, halves):
+            nc.scalar.activation(out=tanh[:, heads, halves], in_=og_raw[:, heads, halves], func=ACT.Tanh, scale=0.5)
 
-        def tanhs(hs, us):
-            nc.scalar.activation(out=tanh[:, hs, us], in_=og_raw[:, hs, us], func=ACT.Tanh, scale=0.5)
-
-        def gates(hs, us):
-            nc.scalar.activation(out=gate[:, hs, us], in_=tanh[:, hs, us], func=ACT.Copy, scale=0.5, bias=0.5)
+        def gate_affine(heads, halves):
+            nc.scalar.activation(
+                out=gate[:, heads, halves], in_=tanh[:, heads, halves], func=ACT.Copy, scale=0.5, bias=0.5
+            )
 
         def denominators(n):
-            first, last = PAIRS[n // 2]
+            size = len(GROUPS[n])
+            (first, half), last = UNITS[GROUPS[n][0]], UNITS[GROUPS[n][-1]][0]
+            heads = slice(first, last + 1, max(last - first, 1))
             nc.vector.tensor_tensor(
-                out=den[n][:],
-                in0=y[n][:, :, :, E - 1],
-                in1=sink_cols[:, n % 2, :, first : last + 1 : last - first].rearrange("p c g -> p g c"),
+                out=den[n][:, :size],
+                in0=y[n % Y_BANKS][:, :size, :, E - 1],
+                in1=sink_cols[:, half, :, heads].rearrange("m c h -> m h c"),
                 op=ALU.add,
             )
 
-        def denominator(i):
-            nc.vector.tensor_tensor(
-                out=den[i - 3][:, i % 2], in0=y_of(i)[:, :, E - 1], in1=sink_cols[:, 1, :, head_of(i)], op=ALU.add
-            )
-
         def invert(n):
-            nc.vector.reciprocal(out=rden[n][:], in_=den[n][:])
+            size = len(GROUPS[n])
+            nc.vector.reciprocal(out=rden[n][:, :size], in_=den[n][:, :size])
 
-        def invert_one(i):
-            nc.vector.reciprocal(out=rden[i - 3][:, i % 2], in_=den[i - 3][:, i % 2])
-
-        def finish(i, parts=(0, 1)):
-            slot = i - 3 if i >= 6 else i // 2
-            for c in parts:
+        def finish(i):
+            h, half = UNITS[i]
+            n = GROUP_OF[i]
+            for c in range(2):
                 nc.vector.scalar_tensor_tensor(
                     out=res[i][:, c, :],
-                    in0=y_of(i)[:, c, :],
-                    scalar=rden[slot][:, i % 2, c : c + 1],
-                    in1=gate[:, head_of(i), UNITS[i][1], c * E : (c + 1) * E],
+                    in0=y_place(i)[:, c, :],
+                    scalar=rden[n][:, GROUPS[n].index(i), c : c + 1],
+                    in1=gate[:, h, half, c * E : (c + 1) * E],
                     op0=ALU.mult,
                     op1=ALU.mult,
                 )
-            half = UNITS[i][1]
-            if 1 in parts:
-                nc.sync.dma_start(
-                    out=out[head_of(i), half * HALF : (half + 1) * HALF, :].rearrange("(m c) e -> m c e", c=2),
-                    in_=res[i][:],
-                )
+            nc.sync.dma_start(
+                out=out[h, half * HALF : (half + 1) * HALF, :].rearrange("(m c) e -> m c e", c=2), in_=res[i][:]
+            )
+
+        both_halves = slice(0, 2)
+        middle_heads = slice(1, 3)
+
+        nc.gpsimd.memset(warm_in[:], 1.0)
+        nc.gpsimd.memset(k_mx[0][:, N:], 0)
+        nc.gpsimd.memset(sink_rows[:], 0.0)
+        nc.scalar.dma_start(out=t_raw[:], in_=t.rearrange("(s r) o -> s (r o)", r=PACK))
+        nc.scalar.dma_start(out=kb_raw[:], in_=kb.rearrange("(s r) o -> s (r o)", r=PACK))
+        nc.sync.dma_start(out=k_raw[:], in_=kT.rearrange("g (p j) n -> (g p) j n", j=PACK))
+        for n in range(4):
+            load_q(n)
+        load_og(0)
+        nc.sync.dma_start(
+            out=v_raw[:].rearrange("p g r e -> p g (r e)"), in_=v.rearrange("g (s r) e -> s g (r e)", r=PACK)
+        )
 
         nc.scalar.activation(out=warm_out[0][:], in_=warm_in[:], func=ACT.Ln)
-        nc.vector.tensor_scalar(out=mant[:], in0=t_raw[:].bitcast(I32), scalar1=MANTISSA, scalar2=ONE_BITS, op0=ALU.bitwise_and, op1=ALU.bitwise_or)
-        nc.vector.tensor_scalar(out=expo[:], in0=t_raw[:].bitcast(I32), scalar1=23, scalar2=0xFF, op0=ALU.logical_shift_right, op1=ALU.bitwise_and)
-        nc.vector.tensor_scalar(out=sign[:, 0, 0, :], in0=t_raw[:].bitcast(I32), scalar1=SIGN_BIT, scalar2=ONE_BITS, op0=ALU.bitwise_and, op1=ALU.bitwise_or)
-        nc.scalar.activation(out=mant_ln[:], in_=mant[:].bitcast(F32), func=ACT.Ln)
+        t_bits = t_raw[:].bitcast(I32)
+        nc.vector.tensor_scalar(
+            out=mantissa[:], in0=t_bits, scalar1=MANTISSA_MASK, scalar2=ONE_BITS, op0=ALU.bitwise_and, op1=ALU.bitwise_or
+        )
+        nc.vector.tensor_scalar(
+            out=exponent[:],
+            in0=t_bits,
+            scalar1=EXPONENT_SHIFT,
+            scalar2=EXPONENT_MASK,
+            op0=ALU.logical_shift_right,
+            op1=ALU.bitwise_and,
+        )
+        nc.vector.tensor_scalar(
+            out=sign[:, 0, 0, :], in0=t_bits, scalar1=SIGN_MASK, scalar2=ONE_BITS, op0=ALU.bitwise_and, op1=ALU.bitwise_or
+        )
+        nc.scalar.activation(out=ln_mantissa[:], in_=mantissa[:].bitcast(F32), func=ACT.Ln)
         nc.scalar.activation(out=warm_out[1][:], in_=warm_in[:], func=ACT.Exp)
-        nc.vector.tensor_scalar(out=expo_ln[:], in0=expo[:], scalar1=-127.0, scalar2=math.log(2.0), op0=ALU.add, op1=ALU.mult)
-        cast_q(0)
-        nc.vector.tensor_tensor(out=bias_part[:], in0=expo_ln[:], in1=kb_raw[:], op=ALU.add)
-        quant_q(0)
-        nc.vector.tensor_tensor(out=bias[:], in0=bias_part[:], in1=mant_ln[:], op=ALU.add)
-        cast_k(0, 3, 4, nc.scalar.copy)
-        cast_k(0, 0, 3)
-        cast_k(1, 3, 4, nc.scalar.copy)
-        cast_k(1, 0, 1)
-        cast_k(1, 1, 2)
+        nc.vector.tensor_scalar(
+            out=ln_power[:], in0=exponent[:], scalar1=-EXPONENT_BIAS, scalar2=math.log(2.0), op0=ALU.add, op1=ALU.mult
+        )
+        nc.vector.tensor_tensor(out=bias_part[:], in0=ln_power[:], in1=kb_raw[:], op=ALU.add)
+        nc.vector.tensor_tensor(out=bias[:], in0=bias_part[:], in1=ln_mantissa[:], op=ALU.add)
+
+        cast_k(2, nc.scalar.copy)
+        cast_k(3, nc.scalar.copy)
+        cast_k(0, nc.vector.tensor_copy)
+        cast_k(1, nc.vector.tensor_copy)
         quant_k(0)
-        scores(0, 0)
-        cast_k(1, 2, 3)
+        cast_q(0)
         quant_k(1)
-        scores(0, 1)
-        cast_q(1)
+        quant_q(0)
+        scores([0], [0, 1])
         quant_k(2)
+        cast_q(1)
         quant_k(3)
         quant_q(1)
-        weights(0, 0)
-        scores(0, 2)
-        weights(0, 1)
-        scores(0, 3)
-        weights(0, 2)
-        scores(1, 0)
-        weights(0, 3)
-        scores(1, 1)
-        cast_v()
-        nc.vector.tensor_copy(out=sink_dealt[:], in_=sink_rows[:].rearrange("p u (n c) -> p u c n", c=2))
-        group_w(0)
-        quantize(v_codes, v_scales, v_bf[:].rearrange("p g e j -> p (g e j)"))
+        for g in range(2):
+            swap_keys(g)
+        load_og(3)
+        for h in range(H):
+            load_sink(h)
+        load_og(1)
+        load_og(2)
+
+        weights([0], [0])
+        scores([0], [2])
+        weights([0], [1])
+        scores([0], [3])
+        scores([1], range(PACK))
+        weights([0], [2, 3])
         cast_q(2)
-        quant_w(0)
-        group_w(1)
         quant_q(2)
-        turn_sink()
-        quant_w(1)
-        weights(1, 0)
-        scores(1, 2)
-        weights(1, 1)
-        scores(1, 3)
-        weights(1, 2)
-        weights(1, 3)
-        scores(2, 0)
-        scores(2, 1)
-        values(0)
-        values(1)
-        tanhs(heads(0), slice(0, 2))
-        group_w(2)
+        scores([2], range(PACK))
+        weights([1], range(PACK))
+        group_w(0)
         cast_q(3)
-        quant_w(2)
-        denominators(0)
+        quant_w(0)
         quant_q(3)
+        scores([3], range(PACK))
+        gate_tanh(0, both_halves)
+        weights([2], range(PACK))
+        group_w(1)
+        cast_v()
+        quant_w(1)
+        quant_v()
+        weights([3], [0, 1])
+        scores([4, 5], [0])
+        weights([3], [2, 3])
+        scores([4, 5], [1])
+        gate_affine(0, both_halves)
+        group_w(2)
         group_w(3)
-        invert(0)
+        quant_w(2)
+        nc.vector.tensor_copy(out=sink_dealt[:], in_=sink_rows[:].rearrange("p u (n c) -> p u c n", c=2))
         quant_w(3)
-        weights(2, 0)
-        scores(2, 2)
-        weights(2, 1)
-        scores(2, 3)
+        nc.vector.transpose(
+            out=sink_cols[:].rearrange("p u c h -> p (u c h)"), in_=sink_dealt[:].rearrange("p u c n -> p (u c n)")
+        )
+
+        weights([4, 5], [0])
+        values(0)
+        scores([4, 5], [2])
+        weights([4, 5], [1])
+        values(1)
+        scores([4, 5], [3])
+        weights([4, 5], [2])
+        scores([6, 7], [0, 1])
+        weights([4, 5], [3])
         values(2)
-        weights(2, 2)
-        weights(2, 3)
-        scores(3, 0)
-        scores(3, 1)
+        scores([6, 7], [2, 3])
         values(3)
-        scores(3, 2)
-        scores(3, 3)
-        gates(heads(0), slice(0, 2))
-        tanhs(heads(1), 0)
+        gate_tanh(3, both_halves)
+        weights([6], range(PACK))
+        gate_affine(3, both_halves)
+        weights([7], range(PACK))
+        for half in range(2):
+            gate_tanh(middle_heads, half)
+        for half in range(2):
+            gate_affine(middle_heads, half)
+
         group_w(4)
+        denominators(0)
         group_w(5)
+        invert(0)
+        denominators(1)
         quant_w(4)
         values(4)
-        denominators(1)
+        invert(1)
         quant_w(5)
         values(5)
-        invert(1)
         finish(0)
-        finish(1)
         finish(2)
-        for g in range(2):
-            for r in range(PACK): weight(3, g, r)
-        gates(heads(1), 0)
-        group_w(7, 128, 256, nc.scalar.copy)
-        tanhs(heads(1), 1)
-        gates(heads(1), 1)
         group_w(6)
         denominators(2)
-        finish(3)
+        finish(1)
         quant_w(6)
         values(6)
-        group_w(7, 0, 128)
+        group_w(7)
         invert(2)
+        finish(3)
         quant_w(7)
         values(7)
-        denominator(6)
+        denominators(3)
         finish(4)
-        invert_one(6)
-        denominator(7)
+        invert(3)
+        denominators(4)
         finish(5)
-        invert_one(7)
+        invert(4)
         finish(6)
         finish(7)

@@ -26,11 +26,12 @@ SIGN_MASK = -0x80000000
 ONE_BITS = 0x3F800000
 EXPONENT_SHIFT, EXPONENT_MASK, EXPONENT_BIAS = 23, 0xFF, 127.0
 
-UNITS = [(0, 0), (3, 0), (0, 1), (3, 1), (1, 0), (2, 0), (1, 1), (2, 1)]
+STAGES = [((1, 2), 0), ((1, 2), 1), ((0, 3), 0), ((0, 3), 1)]
+UNITS = [(h, half) for heads, half in STAGES for h in heads]
 GROUPS = [(0, 1), (2, 3), (4, 5), (6,), (7,)]
 GROUP_OF = {unit: n for n, group in enumerate(GROUPS) for unit in group}
 Y_BANKS = 4
-TURN_ABOUT = (0, 4, 5)
+LAST_STAGE = len(STAGES) - 1
 
 
 def tile_rows_a_exp_kb_sink_gate_kernel(tc, qT, kT, t, v, kb, sink, og, out):
@@ -50,21 +51,20 @@ def tile_rows_a_exp_kb_sink_gate_kernel(tc, qT, kT, t, v, kb, sink, og, out):
         kb_raw = tile("kb_raw", [P, PACK], F32)
         mantissa = tile("mantissa", [P, PACK], I32)
         exponent = tile("exponent", [P, PACK], I32)
-        sign = tile("sign", [P, 1, 1, PACK], I32)
+        sign = tile("sign", [P, 1, PACK, 1], I32)
         ln_power = tile("ln_power", [P, PACK], F32)
         ln_mantissa = tile("ln_mantissa", [P, PACK], F32)
         bias_part = tile("bias_part", [P, PACK], F32)
         bias = tile("bias", [P, PACK], F32)
-        warm_in = tile("warm_in", [P, 1], F32)
-        warm_out = tiles("warm_out", 2, [P, 1], F32)
 
         sink_rows = tile("sink_rows", [P, 2, 2 * QUAD], F32)
         sink_dealt = tile("sink_dealt", [P, 2, 2, QUAD], F32)
         sink_cols = tile("sink_cols", [P, 2, 2, QUAD], F32)
 
-        k_raw = tile("k_raw", [P, PACK, N], F32)
+        k_raw = tiles("k_raw", 2, [P, PACK, N // 2], F32)
         k_bf = tile("k_bf", [P, PACK, P, PACK], BF16)
-        k_mx = tiles("k_mx", 2, [P, N + N // PACK], I32)
+        k_codes = tile("k_codes", [P, N], U32)
+        k_scales = tile("k_scales", [P, N], U8)
         q_raw = tiles("q_raw", 4, [P, PACK, HALF], F32)
         q_bf = tiles("q_bf", 4, [P, HALF, PACK], BF16)
         q_codes = tiles("q_codes", 4, [P, HALF], U32)
@@ -77,10 +77,10 @@ def tile_rows_a_exp_kb_sink_gate_kernel(tc, qT, kT, t, v, kb, sink, og, out):
         tanh = tile("tanh", [P, H, 2, 2 * E], F32)
         gate = tile("gate", [P, H, 2, 2 * E], F32)
 
-        w_rows = tiles("w_rows", len(UNITS), [P, PACK, HALF], BF16)
-        w_bf = tiles("w_bf", len(UNITS), [P, HALF, PACK], BF16)
-        w_codes = tiles("w_codes", len(UNITS), [P, HALF], U32)
-        w_scales = tiles("w_scales", len(UNITS), [P, HALF], U8)
+        w_rows = tiles("w_rows", len(STAGES), [P, PACK, 2 * HALF], BF16)
+        w_bf = tiles("w_bf", len(STAGES), [P, 2 * HALF, PACK], BF16)
+        w_codes = tiles("w_codes", len(STAGES), [P, 2 * HALF], U32)
+        w_scales = tiles("w_scales", len(STAGES), [P, 2 * HALF], U8)
         den = tiles("den", len(GROUPS), [P, 2, 2], F32)
         rden = tiles("rden", len(GROUPS), [P, 2, 2], F32)
         res = tiles("res", len(UNITS), [P, 2, E], F32)
@@ -89,8 +89,19 @@ def tile_rows_a_exp_kb_sink_gate_kernel(tc, qT, kT, t, v, kb, sink, og, out):
         y = [ps.tile([P, 2, 2, E], F32, name="y%d" % b) for b in range(Y_BANKS)]
 
         def load_q(n):
-            two_heads = qT[2 * (n % 2) : 2 * (n % 2) + 2].rearrange("g (p j) q -> (g p) j q", j=PACK)
-            nc.sync.dma_start(out=q_raw[n][:], in_=two_heads[:, :, (n // 2) * HALF : (n // 2 + 1) * HALF])
+            (first, last), half = STAGES[n]
+            queries = slice(half * HALF, (half + 1) * HALF)
+            if last == first + 1:
+                two_heads = qT[first : last + 1].rearrange("g (p j) q -> (g p) j q", j=PACK)
+                nc.sync.dma_start(out=q_raw[n][:], in_=two_heads[:, :, queries])
+            else:
+                for g, h in enumerate((first, last)):
+                    one_head = qT[h].rearrange("(p j) q -> p j q", j=PACK)
+                    nc.sync.dma_start(out=q_raw[n][g * ROWS : (g + 1) * ROWS], in_=one_head[:, :, queries])
+
+        def load_k(a):
+            both_heads = kT.rearrange("g (p j) n -> (g p) j n", j=PACK)
+            nc.sync.dma_start(out=k_raw[a][:], in_=both_heads[:, :, a * N // 2 : (a + 1) * N // 2])
 
         def load_og(h):
             nc.sync.dma_start(out=og_raw[:, h], in_=og[h].rearrange("(u m c) e -> m u (c e)", u=2, c=2))
@@ -100,80 +111,86 @@ def tile_rows_a_exp_kb_sink_gate_kernel(tc, qT, kT, t, v, kb, sink, og, out):
                 out=sink_rows[h:P:QUAD], in_=sink[h].rearrange("(u a n) o -> a u (n o)", u=2, n=2 * QUAD)
             )
 
-        def swap_keys(g):
-            nc.sync.dma_start(out=k_mx[1][(1 - g) * ROWS : (2 - g) * ROWS], in_=k_mx[0][g * ROWS : (g + 1) * ROWS])
-
         def quantize(codes, scales, grouped):
             nc.vector.quantize_mx(out=codes.bitcast(FP8X4), scales=scales, in_=grouped)
 
-        def cast_k(r, copy):
-            copy(out=k_bf[:, r], in_=k_raw[:].rearrange("p j (s r) -> p r s j", r=PACK)[:, r])
+        def cast_k(a):
+            nc.vector.tensor_copy(
+                out=k_bf[:].rearrange("p r s j -> p s j r")[:, a * P // 2 : (a + 1) * P // 2],
+                in_=k_raw[a][:].rearrange("p j (s r) -> p s j r", r=PACK),
+            )
 
-        def quant_k(r):
-            cols = slice(r * P, (r + 1) * P)
-            quantize(k_mx[0][:, cols], k_mx[0][:, N:].bitcast(U8)[:, cols], k_bf[:, r].rearrange("p s j -> p (s j)"))
+        def quant_k(lo, hi):
+            cols = slice(lo * P, hi * P)
+            quantize(k_codes[:, cols], k_scales[:, cols], k_bf[:, lo:hi].rearrange("p r s j -> p (r s j)"))
 
         def cast_q(n):
-            nc.vector.tensor_copy(out=q_bf[n][:], in_=q_raw[n][:].rearrange("p j q -> p q j"))
+            nc.vector.tensor_copy(
+                out=q_bf[n][:].rearrange("p (a b) j -> p a j b", b=PACK),
+                in_=q_raw[n][:].rearrange("p j (a b) -> p a j b", b=PACK),
+            )
 
         def quant_q(n):
             quantize(q_codes[n][:], q_scales[n][:], q_bf[n][:].rearrange("p q j -> p (q j)"))
 
-        def cast_v():
+        def cast_v(g):
             nc.vector.tensor_tensor(
-                out=v_bf[:],
-                in0=v_raw[:].rearrange("p g r e -> p g e r"),
-                in1=sign[:].bitcast(F32).to_broadcast([P, KV, E, PACK]),
+                out=v_bf[:, g].rearrange("p (a b) r -> p a r b", b=PACK),
+                in0=v_raw[:, g].rearrange("p r (a b) -> p a r b", b=PACK),
+                in1=sign[:].bitcast(F32).to_broadcast([P, E // PACK, PACK, PACK]),
                 op=ALU.mult,
             )
 
         def quant_v():
             quantize(v_codes[:], v_scales[:], v_bf[:].rearrange("p g e r -> p (g e r)"))
 
-        def score_place(i, r):
-            banks = score[UNITS[i][0] % 2]
-            if i in TURN_ABOUT:
-                return banks[r % 2][:, r // 2, :]
-            return banks[r // 2][:, r % 2, :]
+        unit_cols = [slice(0, HALF), slice(HALF, 2 * HALF)]
+        stage_cols = slice(0, 2 * HALF)
 
-        def score_matmul(i, r, part):
-            h, half = UNITS[i]
-            keys = k_mx[0 if h % 2 == h // 2 else 1]
-            n = 2 * half + h // 2
-            rows = slice(h % 2 * ROWS, (h % 2 + 1) * ROWS)
-            tokens = slice(r * P, (r + 1) * P)
-            queries = slice(part * P, (part + 1) * P)
-            nc.tensor.matmul_mx(
-                out=score_place(i, r)[:, queries],
-                lhsT=keys[rows, tokens].bitcast(FP8X4),
-                lhsT_scale=keys[rows, N:].bitcast(U8)[:, tokens],
-                rhs=q_codes[n][rows, queries].bitcast(FP8X4),
-                rhs_scale=q_scales[n][rows, queries],
-                start=True,
-                stop=True,
+        def score_place(i, r):
+            banks = score[i % 2]
+            if i // 2 == LAST_STAGE:
+                return banks[r // 2][:, r % 2, :]
+            return banks[r % 2][:, 0, :]
+
+        def scores(n, rs):
+            for r in rs:
+                tokens = slice(r * P, (r + 1) * P)
+                for part in range(2):
+                    queries = slice(part * P, (part + 1) * P)
+                    for g in range(2):
+                        rows = slice(g * ROWS, (g + 1) * ROWS)
+                        nc.tensor.matmul_mx(
+                            out=score_place(2 * n + g, r)[:, queries],
+                            lhsT=k_codes[rows, tokens].bitcast(FP8X4),
+                            lhsT_scale=k_scales[rows, tokens],
+                            rhs=q_codes[n][rows, queries].bitcast(FP8X4),
+                            rhs_scale=q_scales[n][rows, queries],
+                            start=True,
+                            stop=True,
+                        )
+
+        def weight(i, r):
+            nc.scalar.activation(
+                out=w_rows[i // 2][:, r, unit_cols[i % 2]].rearrange("p (c m) -> p c m", c=2),
+                in_=score_place(i, r).rearrange("p (m c) -> p c m", c=2),
+                func=ACT.Exp,
+                bias=bias[:, r : r + 1],
             )
 
-        def scores(units, rs):
+        def weights(n, rs):
             for r in rs:
-                for part in range(2):
-                    for i in units:
-                        score_matmul(i, r, part)
+                for g in range(2):
+                    weight(2 * n + g, r)
 
-        def weights(units, rs):
-            for r in rs:
-                for i in units:
-                    nc.scalar.activation(
-                        out=w_rows[i][:, r, :].rearrange("p (c m) -> p c m", c=2),
-                        in_=score_place(i, r).rearrange("p (m c) -> p c m", c=2),
-                        func=ACT.Exp,
-                        bias=bias[:, r : r + 1],
-                    )
+        def group_w(n, cols):
+            nc.vector.tensor_copy(
+                out=w_bf[n][:, cols].rearrange("p (a b) r -> p a r b", b=PACK),
+                in_=w_rows[n][:, :, cols].rearrange("p r (a b) -> p a r b", b=PACK),
+            )
 
-        def group_w(i):
-            nc.vector.tensor_copy(out=w_bf[i][:], in_=w_rows[i][:].rearrange("p r q -> p q r"))
-
-        def quant_w(i):
-            quantize(w_codes[i][:], w_scales[i][:], w_bf[i][:].rearrange("p q r -> p (q r)"))
+        def quant_w(n, cols):
+            quantize(w_codes[n][:, cols], w_scales[n][:, cols], w_bf[n][:, cols].rearrange("p q r -> p (q r)"))
 
         def y_place(i):
             n = GROUP_OF[i]
@@ -182,11 +199,11 @@ def tile_rows_a_exp_kb_sink_gate_kernel(tc, qT, kT, t, v, kb, sink, og, out):
         def values(i):
             features = slice(UNITS[i][0] // 2 * E, (UNITS[i][0] // 2 + 1) * E)
             for c in range(2):
-                queries = slice(c * P, (c + 1) * P)
+                queries = slice(i % 2 * HALF + c * P, i % 2 * HALF + (c + 1) * P)
                 nc.tensor.matmul_mx(
                     out=y_place(i)[:, c, :],
-                    lhsT=w_codes[i][:, queries].bitcast(FP8X4),
-                    lhsT_scale=w_scales[i][:, queries],
+                    lhsT=w_codes[i // 2][:, queries].bitcast(FP8X4),
+                    lhsT_scale=w_scales[i // 2][:, queries],
                     rhs=v_codes[:, features].bitcast(FP8X4),
                     rhs_scale=v_scales[:, features],
                     start=True,
@@ -196,9 +213,12 @@ def tile_rows_a_exp_kb_sink_gate_kernel(tc, qT, kT, t, v, kb, sink, og, out):
         def gate_tanh(heads, halves):
             nc.scalar.activation(out=tanh[:, heads, halves], in_=og_raw[:, heads, halves], func=ACT.Tanh, scale=0.5)
 
-        def gate_affine(heads, halves):
-            nc.scalar.activation(
-                out=gate[:, heads, halves], in_=tanh[:, heads, halves], func=ACT.Copy, scale=0.5, bias=0.5
+        def gate_affine(heads, half):
+            nc.scalar.activation(out=gate[:, heads, half], in_=tanh[:, heads, half], func=ACT.Copy, scale=0.5, bias=0.5)
+
+        def gate_affine_on_vector(heads, half):
+            nc.vector.tensor_scalar(
+                out=gate[:, heads, half], in0=tanh[:, heads, half], scalar1=0.5, scalar2=0.5, op0=ALU.mult, op1=ALU.add
             )
 
         def denominators(n):
@@ -233,22 +253,28 @@ def tile_rows_a_exp_kb_sink_gate_kernel(tc, qT, kT, t, v, kb, sink, og, out):
             )
 
         both_halves = slice(0, 2)
-        middle_heads = slice(1, 3)
+        inner_heads = slice(1, 3)
+        outer_heads = slice(0, H, 3)
 
-        nc.gpsimd.memset(warm_in[:], 1.0)
-        nc.gpsimd.memset(k_mx[0][:, N:], 0)
         nc.gpsimd.memset(sink_rows[:], 0.0)
         nc.scalar.dma_start(out=t_raw[:], in_=t.rearrange("(s r) o -> s (r o)", r=PACK))
         nc.scalar.dma_start(out=kb_raw[:], in_=kb.rearrange("(s r) o -> s (r o)", r=PACK))
-        nc.sync.dma_start(out=k_raw[:], in_=kT.rearrange("g (p j) n -> (g p) j n", j=PACK))
-        for n in range(4):
-            load_q(n)
-        load_og(0)
+        load_q(0)
+        load_k(0)
+        load_k(1)
+        load_q(1)
         nc.sync.dma_start(
             out=v_raw[:].rearrange("p g r e -> p g (r e)"), in_=v.rearrange("g (s r) e -> s g (r e)", r=PACK)
         )
+        load_q(2)
+        load_q(3)
+        load_og(1)
+        load_og(2)
+        for h in range(H):
+            load_sink(h)
+        load_og(0)
+        load_og(3)
 
-        nc.scalar.activation(out=warm_out[0][:], in_=warm_in[:], func=ACT.Ln)
         t_bits = t_raw[:].bitcast(I32)
         nc.vector.tensor_scalar(
             out=mantissa[:], in0=t_bits, scalar1=MANTISSA_MASK, scalar2=ONE_BITS, op0=ALU.bitwise_and, op1=ALU.bitwise_or
@@ -262,118 +288,107 @@ def tile_rows_a_exp_kb_sink_gate_kernel(tc, qT, kT, t, v, kb, sink, og, out):
             op1=ALU.bitwise_and,
         )
         nc.vector.tensor_scalar(
-            out=sign[:, 0, 0, :], in0=t_bits, scalar1=SIGN_MASK, scalar2=ONE_BITS, op0=ALU.bitwise_and, op1=ALU.bitwise_or
+            out=sign[:, 0, :, 0], in0=t_bits, scalar1=SIGN_MASK, scalar2=ONE_BITS, op0=ALU.bitwise_and, op1=ALU.bitwise_or
         )
         nc.scalar.activation(out=ln_mantissa[:], in_=mantissa[:].bitcast(F32), func=ACT.Ln)
-        nc.scalar.activation(out=warm_out[1][:], in_=warm_in[:], func=ACT.Exp)
         nc.vector.tensor_scalar(
             out=ln_power[:], in0=exponent[:], scalar1=-EXPONENT_BIAS, scalar2=math.log(2.0), op0=ALU.add, op1=ALU.mult
         )
+        cast_q(0)
         nc.vector.tensor_tensor(out=bias_part[:], in0=ln_power[:], in1=kb_raw[:], op=ALU.add)
+        quant_q(0)
         nc.vector.tensor_tensor(out=bias[:], in0=bias_part[:], in1=ln_mantissa[:], op=ALU.add)
 
-        cast_k(2, nc.scalar.copy)
-        cast_k(3, nc.scalar.copy)
-        cast_k(0, nc.vector.tensor_copy)
-        cast_k(1, nc.vector.tensor_copy)
-        quant_k(0)
-        cast_q(0)
-        quant_k(1)
-        quant_q(0)
-        scores([0], [0, 1])
-        quant_k(2)
+        cast_k(0)
+        cast_k(1)
+        quant_k(0, 1)
+        scores(0, [0])
+        quant_k(1, 2)
+        scores(0, [1])
         cast_q(1)
-        quant_k(3)
+        quant_k(2, PACK)
         quant_q(1)
-        for g in range(2):
-            swap_keys(g)
-        load_og(3)
-        for h in range(H):
-            load_sink(h)
-        load_og(1)
-        load_og(2)
 
-        weights([0], [0])
-        scores([0], [2])
-        weights([0], [1])
-        scores([0], [3])
-        scores([1], range(PACK))
-        weights([0], [2, 3])
-        cast_q(2)
-        quant_q(2)
-        scores([2], range(PACK))
-        weights([1], range(PACK))
-        group_w(0)
-        cast_q(3)
-        quant_w(0)
-        quant_q(3)
-        scores([3], range(PACK))
-        gate_tanh(0, both_halves)
-        weights([2], range(PACK))
-        group_w(1)
-        cast_v()
-        quant_w(1)
+        weights(0, [0])
+        scores(0, [2])
+        weights(0, [1])
+        scores(0, [3])
+        weights(0, [2])
+        scores(1, [0])
+        weights(0, [3])
+        scores(1, [1])
+        cast_v(0)
+        cast_v(1)
+
         quant_v()
-        weights([3], [0, 1])
-        scores([4, 5], [0])
-        weights([3], [2, 3])
-        scores([4, 5], [1])
-        gate_affine(0, both_halves)
-        group_w(2)
-        group_w(3)
-        quant_w(2)
+        group_w(0, unit_cols[0])
+        cast_q(2)
+        quant_w(0, unit_cols[0])
+        quant_q(2)
+        group_w(0, unit_cols[1])
+        cast_q(3)
+        quant_w(0, unit_cols[1])
+        weights(1, [0])
+        scores(1, [2])
+        weights(1, [1])
+        scores(1, [3])
+        weights(1, [2])
+        scores(2, [0])
+        weights(1, [3])
+        scores(2, [1])
+
+        quant_q(3)
+        group_w(1, stage_cols)
         nc.vector.tensor_copy(out=sink_dealt[:], in_=sink_rows[:].rearrange("p u (n c) -> p u c n", c=2))
-        quant_w(3)
+        quant_w(1, stage_cols)
         nc.vector.transpose(
             out=sink_cols[:].rearrange("p u c h -> p (u c h)"), in_=sink_dealt[:].rearrange("p u c n -> p (u c n)")
         )
-
-        weights([4, 5], [0])
+        weights(2, [0])
+        scores(2, [2])
+        weights(2, [1])
+        scores(2, [3])
         values(0)
-        scores([4, 5], [2])
-        weights([4, 5], [1])
         values(1)
-        scores([4, 5], [3])
-        weights([4, 5], [2])
-        scores([6, 7], [0, 1])
-        weights([4, 5], [3])
+        weights(2, [2, 3])
+        scores(LAST_STAGE, range(PACK))
         values(2)
-        scores([6, 7], [2, 3])
         values(3)
-        gate_tanh(3, both_halves)
-        weights([6], range(PACK))
-        gate_affine(3, both_halves)
-        weights([7], range(PACK))
-        for half in range(2):
-            gate_tanh(middle_heads, half)
-        for half in range(2):
-            gate_affine(middle_heads, half)
+        gate_tanh(inner_heads, both_halves)
 
-        group_w(4)
+        for g in range(2):
+            for r in range(PACK):
+                weight(2 * LAST_STAGE + g, r)
+        gate_affine(inner_heads, 1)
+        for half in range(2):
+            gate_tanh(outer_heads, half)
+        for half in range(2):
+            gate_affine(outer_heads, half)
+
+        group_w(2, stage_cols)
         denominators(0)
-        group_w(5)
-        invert(0)
+        gate_affine_on_vector(inner_heads, 0)
         denominators(1)
-        quant_w(4)
+        invert(0)
+        quant_w(2, stage_cols)
         values(4)
-        invert(1)
-        quant_w(5)
         values(5)
+        invert(1)
+        group_w(LAST_STAGE, unit_cols[0])
         finish(0)
-        finish(2)
-        group_w(6)
-        denominators(2)
         finish(1)
-        quant_w(6)
+        quant_w(LAST_STAGE, unit_cols[0])
         values(6)
-        group_w(7)
-        invert(2)
-        finish(3)
-        quant_w(7)
+        group_w(LAST_STAGE, unit_cols[1])
+        denominators(2)
+        finish(2)
+        quant_w(LAST_STAGE, unit_cols[1])
         values(7)
+        invert(2)
         denominators(3)
-        finish(4)
+        finish(3)
         invert(3)
+        finish(4)
         denominators(4)
         finish(5)
         invert(4)

import math
from contextlib import ExitStack

import concourse.mybir as mybir

H, KV, D, NQ, N, E = 4, 2, 256, 512, 512, 128
FLOPS = 2 * H * N * NQ * (D + E)

F32 = mybir.dt.float32
BF16 = mybir.dt.bfloat16
I32 = mybir.dt.int32
U32 = mybir.dt.uint32
U8 = mybir.dt.uint8
FP8X4 = mybir.dt.float8_e4m3fn_x4
ALU = mybir.AluOpType
ACT = mybir.ActivationFunctionType

P = 128
ROWS = 64
PACK = 4
HALF = NQ // 2
QUAD = 32

MANTISSA_MASK = 0x007FFFFF
SIGN_MASK = -0x80000000
ONE_BITS = 0x3F800000
EXPONENT_SHIFT, EXPONENT_MASK, EXPONENT_BIAS = 23, 0xFF, 127.0

STAGES = [((1, 2), 0), ((1, 2), 1), ((0, 3), 0), ((0, 3), 1)]
UNITS = [(h, half) for heads, half in STAGES for h in heads]
GROUPS = [(0, 1), (2, 3), (4, 5), (6,), (7,)]
GROUP_OF = {unit: n for n, group in enumerate(GROUPS) for unit in group}
Y_BANKS = 4
LAST_STAGE = len(STAGES) - 1


def tile_rows_a_exp_kb_sink_gate_kernel(tc, qT, kT, t, v, kb, sink, og, out):
    nc = tc.nc
    with ExitStack() as ctx:
        sb = ctx.enter_context(tc.tile_pool(name="sb", bufs=1))
        ps = ctx.enter_context(tc.psum_pool(name="ps", bufs=1))
        ctx.enter_context(tc.manual_schedule())

        def tile(name, shape, dtype):
            return sb.tile(shape, dtype, name=name, align_bytes=64)

        def tiles(name, count, shape, dtype):
            return [tile("%s%d" % (name, n), shape, dtype) for n in range(count)]

        t_raw = tile("t_raw", [P, PACK], F32)
        kb_raw = tile("kb_raw", [P, PACK], F32)
        mantissa = tile("mantissa", [P, PACK], I32)
        exponent = tile("exponent", [P, PACK], I32)
        sign = tile("sign", [P, 1, PACK, 1], I32)
        ln_power = tile("ln_power", [P, PACK], F32)
        ln_mantissa = tile("ln_mantissa", [P, PACK], F32)
        bias_part = tile("bias_part", [P, PACK], F32)
        bias = tile("bias", [P, PACK], F32)

        sink_rows = tile("sink_rows", [P, 2, 2 * QUAD], F32)
        sink_dealt = tile("sink_dealt", [P, 2, 2, QUAD], F32)
        sink_cols = tile("sink_cols", [P, 2, 2, QUAD], F32)

        k_raw = tiles("k_raw", 2, [P, PACK, N // 2], F32)
        k_bf = tile("k_bf", [P, PACK, P, PACK], BF16)
        k_codes = tile("k_codes", [P, N], U32)
        k_scales = tile("k_scales", [P, N], U8)
        q_raw = tiles("q_raw", 4, [P, PACK, HALF], F32)
        q_bf = tiles("q_bf", 4, [P, HALF, PACK], BF16)
        q_codes = tiles("q_codes", 4, [P, HALF], U32)
        q_scales = tiles("q_scales", 4, [P, HALF], U8)
        v_raw = tile("v_raw", [P, KV, PACK, E], F32)
        v_bf = tile("v_bf", [P, KV, E, PACK], BF16)
        v_codes = tile("v_codes", [P, KV * E], U32)
        v_scales = tile("v_scales", [P, KV * E], U8)
        og_raw = tile("og_raw", [P, H, 2, 2 * E], F32)
        tanh = tile("tanh", [P, H, 2, 2 * E], F32)
        gate = tile("gate", [P, H, 2, 2 * E], F32)

        w_rows = tiles("w_rows", len(STAGES), [P, PACK, 2 * HALF], BF16)
        w_bf = tiles("w_bf", len(STAGES), [P, 2 * HALF, PACK], BF16)
        w_codes = tiles("w_codes", len(STAGES), [P, 2 * HALF], U32)
        w_scales = tiles("w_scales", len(STAGES), [P, 2 * HALF], U8)
        den = tiles("den", len(GROUPS), [P, 2, 2], F32)
        rden = tiles("rden", len(GROUPS), [P, 2, 2], F32)
        res = tiles("res", len(UNITS), [P, 2, E], F32)

        score = [[ps.tile([P, 2, HALF], F32, name="score%d%d" % (g, b)) for b in range(2)] for g in range(2)]
        y = [ps.tile([P, 2, 2, E], F32, name="y%d" % b) for b in range(Y_BANKS)]

        def load_q(n):
            (first, last), half = STAGES[n]
            queries = slice(half * HALF, (half + 1) * HALF)
            if last == first + 1:
                two_heads = qT[first : last + 1].rearrange("g (p j) q -> (g p) j q", j=PACK)
                nc.sync.dma_start(out=q_raw[n][:], in_=two_heads[:, :, queries])
            else:
                for g, h in enumerate((first, last)):
                    one_head = qT[h].rearrange("(p j) q -> p j q", j=PACK)
                    nc.sync.dma_start(out=q_raw[n][g * ROWS : (g + 1) * ROWS], in_=one_head[:, :, queries])

        def load_k(a):
            both_heads = kT.rearrange("g (p j) n -> (g p) j n", j=PACK)
            nc.sync.dma_start(out=k_raw[a][:], in_=both_heads[:, :, a * N // 2 : (a + 1) * N // 2])

        def load_og(h):
            nc.sync.dma_start(out=og_raw[:, h], in_=og[h].rearrange("(u m c) e -> m u (c e)", u=2, c=2))

        def load_sink(h):
            nc.sync.dma_start(
                out=sink_rows[h:P:QUAD], in_=sink[h].rearrange("(u a n) o -> a u (n o)", u=2, n=2 * QUAD)
            )

        def quantize(codes, scales, grouped):
            nc.vector.quantize_mx(out=codes.bitcast(FP8X4), scales=scales, in_=grouped)

        def cast_k(a):
            nc.vector.tensor_copy(
                out=k_bf[:].rearrange("p r s j -> p s j r")[:, a * P // 2 : (a + 1) * P // 2],
                in_=k_raw[a][:].rearrange("p j (s r) -> p s j r", r=PACK),
            )

        def quant_k(lo, hi):
            cols = slice(lo * P, hi * P)
            quantize(k_codes[:, cols], k_scales[:, cols], k_bf[:, lo:hi].rearrange("p r s j -> p (r s j)"))

        def cast_q(n):
            nc.vector.tensor_copy(
                out=q_bf[n][:].rearrange("p (a b) j -> p a j b", b=PACK),
                in_=q_raw[n][:].rearrange("p j (a b) -> p a j b", b=PACK),
            )

        def quant_q(n):
            quantize(q_codes[n][:], q_scales[n][:], q_bf[n][:].rearrange("p q j -> p (q j)"))

        def cast_v(g):
            nc.vector.tensor_tensor(
                out=v_bf[:, g].rearrange("p (a b) r -> p a r b", b=PACK),
                in0=v_raw[:, g].rearrange("p r (a b) -> p a r b", b=PACK),
                in1=sign[:].bitcast(F32).to_broadcast([P, E // PACK, PACK, PACK]),
                op=ALU.mult,
            )

        def quant_v():
            quantize(v_codes[:], v_scales[:], v_bf[:].rearrange("p g e r -> p (g e r)"))

        unit_cols = [slice(0, HALF), slice(HALF, 2 * HALF)]
        stage_cols = slice(0, 2 * HALF)

        def score_place(i, r):
            banks = score[i % 2]
            if i // 2 == LAST_STAGE:
                return banks[r // 2][:, r % 2, :]
            return banks[r % 2][:, 0, :]

        def scores(n, rs):
            for r in rs:
                tokens = slice(r * P, (r + 1) * P)
                for part in range(2):
                    queries = slice(part * P, (part + 1) * P)
                    for g in range(2):
                        rows = slice(g * ROWS, (g + 1) * ROWS)
                        nc.tensor.matmul_mx(
                            out=score_place(2 * n + g, r)[:, queries],
                            lhsT=k_codes[rows, tokens].bitcast(FP8X4),
                            lhsT_scale=k_scales[rows, tokens],
                            rhs=q_codes[n][rows, queries].bitcast(FP8X4),
                            rhs_scale=q_scales[n][rows, queries],
                            start=True,
                            stop=True,
                        )

        def weight(i, r):
            nc.scalar.activation(
                out=w_rows[i // 2][:, r, unit_cols[i % 2]].rearrange("p (c m) -> p c m", c=2),
                in_=score_place(i, r).rearrange("p (m c) -> p c m", c=2),
                func=ACT.Exp,
                bias=bias[:, r : r + 1],
            )

        def weights(n, rs):
            for r in rs:
                for g in range(2):
                    weight(2 * n + g, r)

        def group_w(n, cols):
            nc.vector.tensor_copy(
                out=w_bf[n][:, cols].rearrange("p (a b) r -> p a r b", b=PACK),
                in_=w_rows[n][:, :, cols].rearrange("p r (a b) -> p a r b", b=PACK),
            )

        def quant_w(n, cols):
            quantize(w_codes[n][:, cols], w_scales[n][:, cols], w_bf[n][:, cols].rearrange("p q r -> p (q r)"))

        def y_place(i):
            n = GROUP_OF[i]
            return y[n % Y_BANKS][:, GROUPS[n].index(i)]

        def values(i):
            features = slice(UNITS[i][0] // 2 * E, (UNITS[i][0] // 2 + 1) * E)
            for c in range(2):
                queries = slice(i % 2 * HALF + c * P, i % 2 * HALF + (c + 1) * P)
                nc.tensor.matmul_mx(
                    out=y_place(i)[:, c, :],
                    lhsT=w_codes[i // 2][:, queries].bitcast(FP8X4),
                    lhsT_scale=w_scales[i // 2][:, queries],
                    rhs=v_codes[:, features].bitcast(FP8X4),
                    rhs_scale=v_scales[:, features],
                    start=True,
                    stop=True,
                )

        def gate_tanh(heads, halves):
            nc.scalar.activation(out=tanh[:, heads, halves], in_=og_raw[:, heads, halves], func=ACT.Tanh, scale=0.5)

        def gate_affine(heads, half):
            nc.scalar.activation(out=gate[:, heads, half], in_=tanh[:, heads, half], func=ACT.Copy, scale=0.5, bias=0.5)

        def gate_affine_on_vector(heads, half):
            nc.vector.tensor_scalar(
                out=gate[:, heads, half], in0=tanh[:, heads, half], scalar1=0.5, scalar2=0.5, op0=ALU.mult, op1=ALU.add
            )

        def denominators(n):
            size = len(GROUPS[n])
            (first, half), last = UNITS[GROUPS[n][0]], UNITS[GROUPS[n][-1]][0]
            heads = slice(first, last + 1, max(last - first, 1))
            nc.vector.tensor_tensor(
                out=den[n][:, :size],
                in0=y[n % Y_BANKS][:, :size, :, E - 1],
                in1=sink_cols[:, half, :, heads].rearrange("m c h -> m h c"),
                op=ALU.add,
            )

        def invert(n):
            size = len(GROUPS[n])
            nc.vector.reciprocal(out=rden[n][:, :size], in_=den[n][:, :size])

        def finish(i):
            h, half = UNITS[i]
            n = GROUP_OF[i]
            for c in range(2):
                nc.vector.scalar_tensor_tensor(
                    out=res[i][:, c, :],
                    in0=y_place(i)[:, c, :],
                    scalar=rden[n][:, GROUPS[n].index(i), c : c + 1],
                    in1=gate[:, h, half, c * E : (c + 1) * E],
                    op0=ALU.mult,
                    op1=ALU.mult,
                )
            nc.sync.dma_start(
                out=out[h, half * HALF : (half + 1) * HALF, :].rearrange("(m c) e -> m c e", c=2), in_=res[i][:]
            )

        both_halves = slice(0, 2)
        inner_heads = slice(1, 3)
        outer_heads = slice(0, H, 3)

        nc.gpsimd.memset(sink_rows[:], 0.0)
        nc.scalar.dma_start(out=t_raw[:], in_=t.rearrange("(s r) o -> s (r o)", r=PACK))
        nc.scalar.dma_start(out=kb_raw[:], in_=kb.rearrange("(s r) o -> s (r o)", r=PACK))
        load_q(0)
        load_k(0)
        load_k(1)
        load_q(1)
        nc.sync.dma_start(
            out=v_raw[:].rearrange("p g r e -> p g (r e)"), in_=v.rearrange("g (s r) e -> s g (r e)", r=PACK)
        )
        load_q(2)
        load_q(3)
        load_og(1)
        load_og(2)
        for h in range(H):
            load_sink(h)
        load_og(0)
        load_og(3)

        t_bits = t_raw[:].bitcast(I32)
        nc.vector.tensor_scalar(
            out=mantissa[:], in0=t_bits, scalar1=MANTISSA_MASK, scalar2=ONE_BITS, op0=ALU.bitwise_and, op1=ALU.bitwise_or
        )
        nc.vector.tensor_scalar(
            out=exponent[:],
            in0=t_bits,
            scalar1=EXPONENT_SHIFT,
            scalar2=EXPONENT_MASK,
            op0=ALU.logical_shift_right,
            op1=ALU.bitwise_and,
        )
        nc.vector.tensor_scalar(
            out=sign[:, 0, :, 0], in0=t_bits, scalar1=SIGN_MASK, scalar2=ONE_BITS, op0=ALU.bitwise_and, op1=ALU.bitwise_or
        )
        nc.scalar.activation(out=ln_mantissa[:], in_=mantissa[:].bitcast(F32), func=ACT.Ln)
        nc.vector.tensor_scalar(
            out=ln_power[:], in0=exponent[:], scalar1=-EXPONENT_BIAS, scalar2=math.log(2.0), op0=ALU.add, op1=ALU.mult
        )
        cast_q(0)
        nc.vector.tensor_tensor(out=bias_part[:], in0=ln_power[:], in1=kb_raw[:], op=ALU.add)
        quant_q(0)
        nc.vector.tensor_tensor(out=bias[:], in0=bias_part[:], in1=ln_mantissa[:], op=ALU.add)

        cast_k(0)
        cast_k(1)
        quant_k(0, 1)
        scores(0, [0])
        quant_k(1, 2)
        scores(0, [1])
        cast_q(1)
        quant_k(2, PACK)
        quant_q(1)

        weights(0, [0])
        scores(0, [2])
        weights(0, [1])
        scores(0, [3])
        weights(0, [2])
        scores(1, [0])
        weights(0, [3])
        scores(1, [1])
        cast_v(0)
        cast_v(1)

        quant_v()
        group_w(0, unit_cols[0])
        cast_q(2)
        quant_w(0, unit_cols[0])
        quant_q(2)
        group_w(0, unit_cols[1])
        cast_q(3)
        quant_w(0, unit_cols[1])
        weights(1, [0])
        scores(1, [2])
        weights(1, [1])
        scores(1, [3])
        weights(1, [2])
        scores(2, [0])
        weights(1, [3])
        scores(2, [1])

        quant_q(3)
        group_w(1, stage_cols)
        nc.vector.tensor_copy(out=sink_dealt[:], in_=sink_rows[:].rearrange("p u (n c) -> p u c n", c=2))
        quant_w(1, stage_cols)
        nc.vector.transpose(
            out=sink_cols[:].rearrange("p u c h -> p (u c h)"), in_=sink_dealt[:].rearrange("p u c n -> p (u c n)")
        )
        weights(2, [0])
        scores(2, [2])
        weights(2, [1])
        scores(2, [3])
        values(0)
        values(1)
        weights(2, [2, 3])
        scores(LAST_STAGE, range(PACK))
        values(2)
        values(3)
        gate_tanh(inner_heads, both_halves)

        for g in range(2):
            for r in range(PACK):
                weight(2 * LAST_STAGE + g, r)
        gate_affine(inner_heads, 1)
        for half in range(2):
            gate_tanh(outer_heads, half)
        for half in range(2):
            gate_affine(outer_heads, half)

        group_w(2, stage_cols)
        denominators(0)
        gate_affine_on_vector(inner_heads, 0)
        denominators(1)
        invert(0)
        quant_w(2, stage_cols)
        values(4)
        values(5)
        invert(1)
        group_w(LAST_STAGE, unit_cols[0])
        finish(0)
        finish(1)
        quant_w(LAST_STAGE, unit_cols[0])
        values(6)
        group_w(LAST_STAGE, unit_cols[1])
        denominators(2)
        finish(2)
        quant_w(LAST_STAGE, unit_cols[1])
        values(7)
        invert(2)
        denominators(3)
        finish(3)
        invert(3)
        finish(4)
        denominators(4)
        finish(5)
        invert(4)
        finish(6)
        finish(7)
